import numpy as np, ml_dtypes
CORES = [2,6,10,14,18,22,26,30]
N = 8
BF = ml_dtypes.bfloat16
def gentries(a):
    return np.ascontiguousarray(a.reshape(8, 16, -1).transpose(0, 2, 1)).reshape(8, -1)
def gtable(e):
    e = np.asarray(e); return np.ascontiguousarray(e.reshape(8, -1, 16).transpose(0, 2, 1)).reshape(128, -1).astype(np.int32)
W, LW, M, K, CAP, RO = 4096, 12, 1024, 192, 160, 3
def h1(v):
    return ((v * v >> 3) + v) & (W - 1)
def h2(v):
    return ((v * v >> 5) + 37 * v + 1) & (W - 1)
def parts(rng):
    X = rng.integers(0, 16, (N, 8, 16, W)); F = rng.integers(0, W, (N, 8, 16, W)); LG = rng.integers(0, M, (N, 8, W))
    for q in range(N):
        for g in range(8):
            v = rng.permutation(M)[:7 * M // 10]
            LG[q, g, np.where(rng.random(len(v)) < 0.5, h1(v), h2(v))] = v
    LE = (rng.random((N, 8, W)) < rng.choice(np.array([0.3, 0.5, 0.7, 0.9]), (N, 8, 1))).astype(np.int64)
    XL = rng.integers(0, 16, (N, 8, 16, M)); LF = rng.integers(0, M, (N, 8, 16, M))
    return X, F, LG, LE, XL, LF, rng.integers(0, W, (N, 8, 16, K)), rng.integers(0, 16, (N, 8, 16, K))
def pack(X, F, LG, LE, XL, LF, C, Q):
    def bf(a): return np.ascontiguousarray(a).reshape(N, 128, -1).astype(np.float32).astype(BF)
    F = np.ascontiguousarray(F).reshape(N, 128, W)
    return {"xr": bf(X), "fd": (F[..., :W // 2] + W * F[..., W // 2:]).astype(np.int32), "tg": (2 * LG + LE).astype(np.int32), "xl": bf(XL),
            "lf": np.ascontiguousarray(LF).reshape(N, 128, M).astype(np.int32), "cx": np.stack([gtable(a.transpose(0, 2, 1).reshape(8, -1)) for a in C]), "qx": bf(Q)}
def setup_inputs(rng):
    return pack(*parts(rng))
def setup_inputs_spread(rng):
    X, F, LG, LE, XL, LF, C, Q = parts(rng)
    def small(n): return np.minimum((np.exp2(4.2 * rng.random((N, 8, 1, n))) * rng.random((N, 8, 16, n))).astype(np.int64), 15)
    def low(n, top): return np.minimum((top * rng.random((N, 8, 16, n)) ** rng.choice(np.array([1.0, 2.0, 4.0]), (N, 8, 1, n))).astype(np.int64), top - 1)
    LE = (rng.random((N, 8, W)) < rng.random((N, 8, 1))).astype(np.int64)
    return pack(small(W), low(W, W), LG, LE, small(M), low(M, M), low(K, W), small(K))
def setup_inputs_ends(rng):
    X, F, LG, LE, XL, LF, C, Q = parts(rng); h = W // 2
    def faces(n):
        kind = rng.integers(0, 3, (N, 8, 1, n)); a = 15 * np.where(kind == 2, rng.integers(0, 2, (N, 8, 16, n)), kind)
        near = (rng.random((N, 8, 1, n)) < 0.25) & (np.arange(16)[:, None] == rng.integers(0, 16, (N, 8, 1, n)))
        return np.abs(a - near.astype(np.int64))
    def ends(a, top): return np.where(rng.random(a.shape) < 0.66, top * rng.integers(0, 2, a.shape), a)
    X, XL, Q = faces(W), faces(M), faces(K)
    X[..., 0] = 0; X[..., W - 1] = 0; X[..., 1] = 15; X[..., W - 2] = 15
    X[..., 2] = 0; X[..., 0, 2] = 1; X[..., W - 3] = 0; X[..., 15, W - 3] = 1
    m = rng.random((N, 8, 16, h)) < 0.66; e = (W - 1) * rng.integers(0, 2, m.shape)
    F = np.concatenate([np.where(m, e, F[..., :h]), np.where(m, e, F[..., h:])], axis=-1)
    m = rng.random((N, 8, W)) < 0.66; e = (rng.random((N, 8, W)) < 0.6).astype(np.int64)
    LG = np.where(m, (M - 1) * e, LG); LE = np.where(m, e, LE)
    LG[..., 0] = 0; LE[..., 0] = 0; LG[..., W - 1] = M - 1; LE[..., W - 1] = 1
    LF = ends(LF, M - 1); C = ends(C, W - 1)
    for k in (0, 1, K - 1): Q[..., k] = 15; C[..., k] = (W - 1) * rng.integers(0, 2, (N, 8, 16))
    Q[..., K - 2] = 0; C[..., K - 2] = (W - 1) * rng.integers(0, 2, (N, 8, 16))
    for k in (2, K - 3): Q[..., k] = 0; C[..., :15, k] = 1; C[..., 15, k] = W - 1
    for k, v in ((3, 2), (K - 4, W - 3)): Q[..., k] = 15; C[..., :15, k] = (W - 1) * rng.integers(0, 2, (N, 8, 15)); C[..., 15, k] = v
    return pack(X, F, LG, LE, XL, LF, C, Q)
def setup_inputs_corners(rng):
    X, F, LG, LE, XL, LF, C, Q = parts(rng); cnt = (0, 1, CAP - 1, CAP, CAP + 1, K); a = np.arange(M)
    for g in (2, 7):
        LG[:, g] = LG[0, g]; res = a[(LG[0, g][h1(a)] == a) | (LG[0, g][h2(a)] == a)]; LF[:, g] = rng.choice(res, (N, 16, M))
    v = LG[:, 3]; c = np.arange(W)
    for _ in range(3): v = np.where((h1(v) == c) | (h2(v) == c), (v + 1) % M, v)
    LG[:, 3] = v
    few = np.array([0, 1, M - 2, M - 1]); LF[:, 5] = rng.choice(few, (N, 16, M)); LG[:, 6] = rng.choice(few, (N, W))
    LE[:, 4] = 1; LE[0, 0] = 0
    for q in range(N):
        for g in range(8):
            b = rng.permutation(W)[:4 * K].reshape(K, 4)
            C[q, g] = b[np.arange(K)[None, :], rng.integers(0, 4, (16, K))]
            ask = np.zeros(K, np.int64); ask[rng.permutation(K)[:cnt[(q + g) % 6]]] = 1
            if g == 7:
                o = C[q, g][np.argmin(far(X[q, g], C[q, g], Q[q, g]), axis=0), np.arange(K)]; LE[q, g] = 0; LE[q, g, o] = ask
            else: LE[q, g, b] = ask[:, None]
    return pack(X, F, LG, LE, XL, LF, C, Q)
def setup_inputs_ties(rng):
    X, F, LG, LE, XL, LF, C, Q = parts(rng)
    pal = rng.integers(6, 10, (N, 8, 16, 6))
    X = np.take_along_axis(pal, rng.integers(0, 6, (N, 8, 1, W)), 3); XL = np.take_along_axis(pal, rng.integers(0, 6, (N, 8, 1, M)), 3)
    for q in range(N):
        for g in range(8):
            v = rng.permutation(M)[:M // 2]; LG[q, g, h2(v)] = v; LG[q, g, h1(v)] = v
    return pack(X, F, LG, LE, XL, LF, C, Q)
def setup_inputs_alike(rng):
    X, F, LG, LE, XL, LF, C, Q = parts(rng)
    for g in range(8):
        s = rng.permutation(M); w = s[:64]; pl = np.concatenate([h1(w), h2(w)])
        pair = s[:6]; few = np.concatenate([pair, pair ^ 1])
        for q in range(N):
            if g % 2 == 0:
                pool = rng.permutation(W)[:40]; C[q, g] = rng.choice(pool, (16, K)); F[q, g, :, ::2] = rng.choice(pool, (16, W // 2))
                LE[q, g, pool] = rng.random(40) < 0.8; LG[q, g, pool] = rng.choice(few, 40); LF[q, g] = rng.choice(s[:24], (16, M))
            else:
                C[q, g] = rng.choice(pl, (16, K)); LE[q, g, pl] = 1; LG[q, g, pl] = rng.choice(s[64:], 128); LF[q, g] = rng.choice(w, (16, M))
    return pack(X, F, LG, LE, XL, LF, C, Q)
def check_inputs(d):
    bad = []
    for k, lo, hi in (("xr", 0, 15), ("fd", 0, W * W - 1), ("tg", 0, 2 * M - 1), ("xl", 0, 15), ("lf", 0, M - 1), ("cx", 0, W - 1), ("qx", 0, 15)):
        a = np.asarray(d[k]).astype(np.float64)
        if not (np.min(a) >= lo and np.max(a) <= hi): bad.append("range of " + k)
        elif np.any(a != np.floor(a)): bad.append("whole numbers of " + k)
    return bad
def lowest(key, use):
    ix = np.flatnonzero(use); m = np.zeros(len(key), bool); m[ix[np.unique(key[ix], return_index=True)[1]]] = True
    return m
def far(x, c, q):
    return np.add.reduce(np.abs(x[:, c] - q[:, None, :]), axis=0)
def reference(xr, fd, tg, xl, lf, cx, qx):
    def whole(a): return a.astype(np.float32).astype(np.int64).reshape(N, 8, 16, -1)
    X, XL, Q = whole(xr), whole(xl), whole(qx)
    fi = fd.astype(np.int64); F = np.concatenate([fi & (W - 1), fi >> LW], axis=-1).reshape(N, 8, 16, W)
    LG = tg.astype(np.int64) >> 1; LE = tg.astype(np.int64) & 1; LF = lf.astype(np.int64).reshape(N, 8, 16, M)
    C = np.ascontiguousarray(np.stack([gentries(a) for a in cx]).astype(np.int64).reshape(N, 8, K, 16).transpose(0, 1, 3, 2))
    lane = np.arange(K)
    for t in range(RO):
        asked = {}; back = {}
        for r in range(N):
            for g in range(8):
                c = C[r, g]; o = c[np.argmin(far(X[r, g], c, Q[r, g]), axis=0), lane]
                s = np.flatnonzero(lowest(o, LE[r, g][o] == 1))[:CAP]
                asked[r, g] = (o, s, LG[r, g][o[s]], LG[r, g][c[:, s]])
        for r in range(N):
            p = (r + 1 + t % (N - 1)) % N
            for g in range(8):
                o, s, n, sent = asked[r, g]
                back[r, g] = (XL[p, g][:, n], LF[p, g][:, n])
                w = lowest(n ^ 1, np.ones(len(n), bool)); LF[p, g][:, (n ^ 1)[w]] = sent[:, w]
        for r in range(N):
            for g in range(8):
                o, s, n, sent = asked[r, g]; a, v = back[r, g]; q = Q[r, g][:, s]; j = np.arange(len(s))
                c1, c2 = h1(v), h2(v); in1 = LG[r, g][c1] == v; in2 = LG[r, g][c2] == v
                sh = np.where(in1, c1, np.where(in2, c2, np.where(far(X[r, g], c2, q) > far(X[r, g], c1, q), c2, c1)))
                new = ~(in1 | in2); i = np.argmax(new, axis=0); pl = sh[i, j]; w = lowest(pl, np.any(new, axis=0))
                LG[r, g][pl[w]] = v[i, j][w]; LE[r, g][pl[w]] = 1
                F[r, g][:, o[s]] = sh; X[r, g][:, o[s]] = a; LE[r, g][o[s]] = 0
                C[r, g] = F[r, g][:, o]; Q[r, g] = (Q[r, g] + X[r, g][:, o]) >> 1
    return {"yc": C.reshape(N, 128, K).astype(np.float32), "yq": Q.reshape(N, 128, K).astype(np.float32).astype(BF), "yt": (2 * LG + LE).astype(np.float32), "yl": LF.reshape(N, 128, M).astype(np.float32)}

@@ -1,0 +1,583 @@
+from concourse.mybir import AluOpType as Op, ActivationFunctionType as AF
+
+W, M, K, CAP, RO, N = 4096, 1024, 192, 160, 3, 8
+H = 96
+BIG = 65536.0
+RES = 1048576.0
+NE = 8
+
+_S = "sbuf"
+F32, B16, I32, U16, H16 = "float32", "bfloat16", "int32", "uint16", "float16"
+PACK = {
+    "tf": (F32, (("z", 24), ("lis", 24), ("req", 12), ("rk", 12), ("dwin", 12), ("w1", 12), ("w2", 12), ("w3", 12), ("w4", 12), ("w5", 12), ("w6", 12), ("nrq", 12), ("pls", 12),
+                 ("dm4", 12), ("dm1", 12), ("er", 24), ("lt", 16), ("pmf", 4))),
+    "tl": (U16, (("ln", 12), ("lo", 12), ("ld", 12), ("lcl", 12), ("lm", 12))),
+    "ti": (I32, (("ni", 12), ("ei", 12), ("pari", 12), ("dmi", 12), ("pmi", 4))),
+    "tb": (B16, (("wm", 24), ("wp", 24), ("wm1", 24), ("wm2", 24), ("wp1", 24), ("wp2", 24), ("cand", 12), ("exb", 16))),
+    "cb": (B16, (("idb", 128), ("blb", 128), ("bt", 128), ("dg1", 128), ("sa", 128), ("dgc0", 128), ("dgc1", 128), ("dgc2", 128), ("bm", K), ("ltk", 2048))),
+    "cff": (F32, (("one", 512), ("idf", 128), ("blf", 128), ("btf", 128), ("af0", 128), ("af1", 128), ("af2", 128), ("sam", 384), ("rpf", 512), ("vrf", 384))),
+    "chh": (H16, (("rp", 512), ("rpc", 128), ("vr", 128), ("bi", 384), ("idh", 128))),
+}
+PLACE, SCRATCH = {}, {}
+for _b in PACK:
+    _o = 0
+    for _n, _w in PACK[_b][1]:
+        PLACE[_n] = (_b, _o, _w)
+        _o += _w
+    SCRATCH[_b] = (_S, [128, _o], PACK[_b][0])
+for _d, _l in (
+    (B16, (("xw", W + K), ("pw", W + K), ("pcs", 768), ("xlh", M), ("q", K), ("qb", K), ("qrep", 16 * K), ("ma", 16 * K), ("mb", 16 * K), ("pa", 16 * K), ("pb", 16 * K),
+           ("at", K), ("g1", K), ("v1", K), ("g2", K), ("v2", K), ("row", 512), ("ro2", 512), ("wt", 512), ("xl1", M), ("xl2", M), ("xl3", M))),
+    (I32, (("fw", W + K), ("fdt", 2048), ("tgs", 256), ("pci", 768), ("lfi", M), ("cxi", K), ("sct", K), ("sco", K), ("tt", 2 * K), ("cc", 2 * K), ("dc", K), ("sg", K), ("ia", K), ("ic", 512))),
+    (U16, (("lfu", M), ("lc", K), ("ru", 2 * K), ("ru2", K), ("l1", K), ("l2", K), ("lu1", M), ("lu2", M), ("lu3", M))),
+    (F32, (("lh", M + K), ("qs", K), ("cf", K), ("scd", K), ("sct2", K), ("sq", 2 * K), ("sp", K), ("yts", 512), ("s0", K), ("lw1", M), ("lw2", M + K), ("lw3", M + K),
+           ("msg1", K + 12), ("msg2", K + 12), ("msg3", K + 12), ("up1", K + 12), ("up2", K + 12), ("up3", K + 12), ("hm1", K + 12), ("hm2", K + 12), ("hm3", K + 12))),
+    (H16, (("gt", K), ("gu", K), ("b16", K), ("c16", K))),
+):
+    for _n, _w in _l:
+        SCRATCH[_n] = (_S, [128, _w], _d)
+for _n, _w, _d in (("co", 128, F32), ("t1", 128, F32), ("t2", 64, F32), ("t3", 32, F32), ("t4", 16, I32), ("fi", 16, I32), ("fl", 16, H16), ("sl", 128, F32), ("r1", 128, F32), ("r2", 128, F32), ("u1", 128, F32),
+                   ("u2", 128, F32), ("ub", 128, F32), ("pk", 128, B16), ("kk", 128, F32), ("k2", 128, F32), ("ka", 64, F32), ("kb", 32, F32), ("kc", 16, F32), ("kd", 8, I32), ("fe", 16, I32), ("fg", 16, F32), ("fh", 16, I32), ("fm", 32, H16)):
+    SCRATCH[_n] = (_S, [128, 2, _w], _d)
+SCRATCH["eqo"] = (_S, [128, 12, K], B16)
+SCRATCH["eqt"] = (_S, [128, 12, K], B16)
+for _n in ("psk", "psv"):
+    SCRATCH[_n] = ("psum", [128, 2, 512], F32)
+for _n in ("psm", "psu", "psd", "psg"):
+    SCRATCH[_n] = ("psum", [128, 512], F32)
+SEMAPHORES = ["qv", "qs", "qp", "qg"] + ["ld%d" % j for j in range(20)] + ["ls%d" % j for j in range(12)]
+SEMAPHORES += ["%s%d" % (a, j) for a in ("rl", "rx", "ru", "rh") for j in (1, 2, 3)]
+
+
+def tracker(g, T):
+    Q = {"v": g.vector, "s": g.scalar, "p": g.tensor, "g": g, "d": g.sync}
+    cnt = {"v": 0, "s": 0, "p": 0, "g": 0}
+    known = {q: {} for q in Q}
+    hist, wr, rd, total = {}, {}, {}, {}
+    nd = [0]
+
+    def learn(q, sem, val):
+        if known[q].get(sem, 0) < val:
+            known[q][sem] = val
+        for s2, v2 in hist.get((sem, val), {}).items():
+            if known[q].get(s2, 0) < v2:
+                known[q][s2] = v2
+
+    def deps(q, comp, R, Wt):
+        out = []
+        for k in R:
+            if k in wr:
+                out.append((wr[k], True))
+            if k.startswith("ps"):
+                out += [(x, False) for x in rd.get(k, {}).values()]
+        for k in Wt:
+            if k in wr:
+                out.append((wr[k], False))
+            out += [(x, False) for x in rd.get(k, {}).values()]
+        need = {}
+        for (sem, val, dq), raw in out:
+            if comp and dq == q and q == "p":
+                continue
+            if need.get(sem, 0) < val:
+                need[sem] = val
+        for sem in sorted(need, key=lambda s: -len(hist.get((s, need[s]), {}))):
+            if known[q].get(sem, 0) < need[sem]:
+                Q[q].wait_ge(T.sem[sem], need[sem])
+                learn(q, sem, need[sem])
+
+    def note(ev, q, R, Wt):
+        for k in Wt:
+            wr[k] = ev
+            rd[k] = {}
+        for k in R:
+            rd.setdefault(k, {})[ev[0] if ev[2] is None else q] = ev
+
+    def op(q, fns, R="", Wt=""):
+        R, Wt = R.split(), Wt.split()
+        deps(q, True, R, Wt)
+        for f in fns[:-1]:
+            f()
+        sem = "q" + q
+        cnt[q] += 1
+        fns[-1]().then_inc(T.sem[sem], 1)
+        total[sem] = cnt[q]
+        hist[(sem, cnt[q])] = dict(known[q])
+        if cnt[q] > 1:
+            hist[(sem, cnt[q])][sem] = cnt[q] - 1
+        note((sem, cnt[q], q), q, R, Wt)
+
+    def dma(q, out, in_, R="", Wt=""):
+        R, Wt = R.split(), Wt.split()
+        deps(q, False, R, Wt)
+        sem = "ld%d" % nd[0]
+        nd[0] += 1
+        Q[q].dma_start(out, in_).then_inc(T.sem[sem], 16)
+        total[sem] = 16
+        hist[(sem, 16)] = dict(known[q])
+        note((sem, 16, None), q, R, Wt)
+
+    def before_remote(R, local, n):
+        deps("g", False, R.split(), [])
+        total[local] = n
+        note((local, n, None), "g", R.split(), [])
+
+    def arrives(sem, n, key):
+        total[sem] = n
+        wr[key] = (sem, n, None)
+        rd[key] = {}
+
+    def finish():
+        for sem in total:
+            if known["g"].get(sem, 0) < total[sem]:
+                g.wait_ge(T.sem[sem], total[sem])
+                learn("g", sem, total[sem])
+    return op, dma, before_remote, arrives, finish
+
+
+def rank_program(g, core, T, topo):
+    r = T.rank_of(core)
+    if r is None:
+        return
+    v, s, p = g.vector, g.scalar, g.tensor
+    op, dma, before_remote, arrives, finish = tracker(g, T)
+
+    def C(n, a=0, b=None, p0=0, p1=128, st=1):
+        bf, o, w = PLACE[n]
+        return T[bf][p0:p1, o + a:o + (w if b is None else b):st]
+
+    def tt(o, a, b, f, R, Wt):
+        op("v", [lambda: v.tensor_tensor(o, a, b, f)], R, Wt)
+
+    def ts(o, a, x, f, R, Wt, y=None, f2=None):
+        if f2 is None:
+            op("v", [lambda: v.tensor_scalar(o, a, x, None, f)], R, Wt)
+        else:
+            op("v", [lambda: v.tensor_scalar(o, a, x, y, f, f2)], R, Wt)
+
+    def cp(o, a, R, Wt):
+        op("v", [lambda: v.tensor_copy(o, a)], R, Wt)
+
+    def fill(o, c, Wt):
+        op("v", [lambda: v.memset(o, c)], "", Wt)
+
+    def act(o, a, R, Wt, f=AF.Identity, **kw):
+        op("s", [lambda: s.activation(o, a, f, **kw)], R, Wt)
+
+    def mm(o, l, x, st, sp):
+        return lambda: p.matmul(o, l, x, st, sp)
+
+    def scan(o, d, R, Wt):
+        op("v", [lambda: v.tensor_tensor_scan(o, T.s0[:], d, 0.0, Op.add, Op.min)], R + " s0", Wt)
+
+    def send(src, key, dst_rank, dst, sem, local):
+        dst_core = T.cores[dst_rank % N]
+        rid, pid = topo.addr(dst_core)[0:2]
+        eng = topo.engines(core, dst_core)[0:NE]
+        before_remote(key, local, len(eng))
+        g.remote_dma(dst, src, T.sem[sem], T.sem[local], pid, rid, sum(1 << e for e in eng))
+
+    PWI = " ".join("pw%d" % c for c in range(8))
+    PW = PWI + " pwr0 pwr1 pwr2 pwd"
+    XW = "xw0 xw1"
+    FW = "fw0 fw1"
+    QR = " ".join("qr%d" % i for i in range(16))
+    dma("d", T.xw[:, 0:2048], T.xr[:, 0:2048], "", "xw0")
+    dma("s", T.tgs[:], T.tg[:], "", "tgs")
+    dma("d", T.xw[:, 2048:W], T.xr[:, 2048:W], "", "xw1")
+    dma("s", T.cxi[:], T.cx[:], "", "cxi")
+    dma("s", T.q[:], T.qx[:], "", "q")
+    dma("s", T.lfi[:], T.lf[:], "", "lfi")
+    dma("d", T.xlh[:], T.xl[:], "", "xlh")
+    dma("d", T.fdt[:], T.fd[:], "", "fdt")
+    fill(C("one"), 1.0, "one")
+    gop = lambda f, R, Wt: op("g", [f], R, Wt)
+    gop(lambda: g.iota(C("pmi", 0, 1), [[0, 1]], 0, 1), "", "pmi")
+    gop(lambda: g.affine_select(C("blf"), C("one", 0, 128), [[-16, 8], [0, 16]], Op.is_ge, 0.0, 0, 1), "one", "blf")
+    gop(lambda: g.affine_select(C("blf"), C("blf"), [[16, 8], [0, 16]], Op.is_ge, 0.0, 15, -1), "blf", "blf")
+    gop(lambda: g.iota(T.ic[:], [[1, 512]], 0, 0), "", "ic")
+    gop(lambda: g.affine_select(C("idf"), C("one", 0, 128), [[-1, 128]], Op.is_equal, 0.0, 0, 1), "one", "idf")
+    gop(lambda: g.iota(T.ia[:], [[-1, K]], 0, 1), "", "ia")
+    gop(lambda: g.affine_select(C("rpf", p1=32), C("one", p1=32), [[-8, 4], [-1, 8], [0, 16]], Op.is_equal, 0.0, 0, 1), "one", "rpf")
+    gop(lambda: g.affine_select(C("btf"), C("blf"), [[1, 128]], Op.is_ge, 0.0, 0, -1), "blf", "btf")
+    gop(lambda: g.iota(C("dmi"), [[16, 12]], 0, 0), "", "dmi")
+
+    def gaff(t):
+        gop(lambda: g.affine_select(C("af%d" % t), C("one", 0, 128), [[-1, 128]], Op.is_equal, 0.0, -(2 + t), 1), "one", "af%d" % t)
+    for t in range(RO):
+        gaff(t)
+    E = lambda i: C("er", i, i + 1)
+    b8 = C("blf", st=16)
+    ts(C("pmi", 0, 1), C("pmi", 0, 1), 15, Op.bitwise_and, "pmi", "pmi")
+    cp(C("pmf", 0, 1), C("pmi", 0, 1), "pmi", "pmf")
+    PM = C("pmf", 0, 1)
+    ts(T.ic[:], T.ic[:], 15, Op.bitwise_and, "ic", "ic")
+    ts(C("sam", 0, 128), T.ic[:, 0:128], 3.0, Op.is_equal, "ic", "sam0")
+    tt(C("sa"), C("blf"), C("sam", 0, 128), Op.mult, "blf sam0", "sa")
+    for j in range(7):
+        ts(E(j), PM, float(j), Op.is_equal, "pmf", "er%d" % j)
+    ts(E(8), E(0), 32.0, Op.mult, "er0", "er8")
+    ts(E(12), E(3), 32768.0, Op.mult, "er3", "er12")
+    tt(E(9), E(8), E(1), Op.add, "er8 er1", "er9")
+    ts(E(7), E(3), 65536.0, Op.mult, "er3", "er7")
+    ts(E(10), E(9), 2.0, Op.mult, "er9", "er10")
+    ts(E(18), E(3), -1.0, Op.mult, "er3", "er18")
+    tt(E(11), E(10), E(2), Op.add, "er10 er2", "er11")
+    ts(C("lt"), T.ic[:, 0:16], PM, Op.is_gt, "ic pmf", "lt")
+    tt(E(13), E(12), E(11), Op.add, "er12 er11", "er13")
+    act(C("wm", 0, 8), b8, "blf", "wm", scale=-65536.0)
+    act(C("wm", 8, 16), b8, "blf", "wm", scale=-131072.0)
+    act(C("wm", 16, 24), b8, "blf", "wm", scale=0.0)
+    act(C("wp", 0, 8), b8, "blf er13", "wp", scale=E(13))
+    act(C("wp", 8, 16), b8, "blf er7", "wp", scale=E(7))
+    act(C("wp", 16, 24), b8, "blf er9", "wp", scale=E(9))
+    ts(T.pci[:, 0:256], T.tgs[:], 6, Op.logical_shift_right, "tgs", "pci0")
+    ts(T.pci[:, 256:512], T.tgs[:], 1, Op.logical_shift_right, "tgs", "pci1", 31, Op.bitwise_and)
+    ts(T.pci[:, 512:768], T.tgs[:], 1, Op.bitwise_and, "tgs", "pci2")
+    cp(T.pcs[:], T.pci[:], "pci0 pci1 pci2", "pcs")
+    fill(T.pw[:, W:W + K], 0.0, "pwd")
+    cp(T.lc[:], T.cxi[:], "cxi", "lc")
+    cp(T.cf[:], T.cxi[:], "cxi", "cf")
+    ts(T.c16[:], T.cxi[:], -2048.0, Op.add, "cxi", "c16")
+    for i in range(16):
+        if i % 2:
+            act(T.qrep[:, i:16 * K:16], T.q[:], "q", "qr%d" % i)
+        else:
+            cp(T.qrep[:, i:16 * K:16], T.q[:], "q", "qr%d" % i)
+    banks = (("psk0", T.psk[:, 0, :]), ("psk1", T.psk[:, 1, :]), ("psv0", T.psv[:, 0, :]), ("psv1", T.psv[:, 1, :]), ("psm", T.psm[:]), ("psu", T.psu[:]), ("psd", T.psd[:]), ("psg", T.psg[:]))
+    for c in range(8):
+        bk, ap = banks[c]
+        op("p", [mm(ap, C("sa"), T.xw[:, 512 * c:512 * c + 512], True, True)], "sa xw%d" % (c // 4), bk)
+        if c % 2:
+            cp(T.pw[:, 512 * c:512 * c + 512], ap, bk, "pw%d" % c)
+        else:
+            act(T.pw[:, 512 * c:512 * c + 512], ap, bk, "pw%d" % c)
+    for j in range(3):
+        dma("d", T.pw[j:128:16, 0:W], T.pcs[:, 256 * j:256 * j + 256], "pcs " + PWI, "pwr%d" % j)
+
+    def weights():
+        fill(T.row[:], 0.0, "row")
+        ts(T.row[0:1, 0:128], T.ic[0:1, 0:128], 2048.0, Op.mult, "ic", "row")
+        ts(T.row[0:1, 128:256], T.ic[0:1, 0:128], 4096.0, Op.mult, "ic", "row", 2048.0, Op.add)
+        fill(T.ro2[:], 1.0, "ro2")
+        cp(C("idh"), C("idf"), "idf", "idh")
+
+    def scalar_later():
+        act(C("idb"), C("idf"), "idf", "idb")
+        for nm, cols in (("wm1", (2.0, 0.0, 0.0)), ("wm2", (-2.0, 0.0, 0.0)), ("wp1", (18, 9, 0.0)), ("wp2", (3, 0.0, 9))):
+            for j, w in enumerate(cols):
+                if w in (18, 9, 3):
+                    act(C(nm, 8 * j, 8 * j + 8), b8, "blf er%d" % w, nm, scale=E(w))
+                else:
+                    act(C(nm, 8 * j, 8 * j + 8), b8, "blf", nm, scale=w)
+        act(C("blb"), C("blf"), "blf", "blb")
+        act(C("bt"), C("btf"), "btf", "bt")
+        for k in range(16):
+            act(C("ltk", 128 * k, 128 * k + 128), C("blf"), "blf lt", "ltk", scale=C("lt", k, k + 1))
+
+    def later():
+        cp(C("rp", p1=32), C("rpf", p1=32), "rpf", "rp")
+        ts(T.ia[:], T.ia[:], 15, Op.bitwise_and, "ia", "ia")
+        ts(C("bm"), T.ia[:], 0.0, Op.not_equal, "ia", "bm", BIG, Op.mult)
+        ts(T.s0[:], T.ic[:, 0:K], 0.0, Op.is_equal, "ic", "s0", RES, Op.mult)
+        for j, w in enumerate((-1.0, -1.0, 2.0)):
+            ts(C("bi", 128 * j, 128 * j + 128), C("idf"), w, Op.mult, "idf", "bi")
+        ts(T.row[32:33, 384:512], T.ic[32:33, 0:128], 2048.0, Op.mult, "ic row", "row1")
+
+    def latest():
+        ts(C("dm4"), C("dmi"), PM, Op.add, "dmi pmf", "dm4", float(W), Op.add)
+        ts(C("dm1"), C("dmi"), PM, Op.add, "dmi pmf", "dm1", float(M), Op.add)
+        fill(C("exb"), 0.0, "exb")
+
+    def claim_weights():
+        ts(T.row[0:1, 384:512], T.ic[0:1, 0:128], 2.0, Op.is_equal, "ic row", "row2")
+        for t in range(RO):
+            ts(T.row[96:97, 128 * t:128 * t + 128], T.ic[96:97, 0:128], 4.0 + t, Op.is_equal, "ic row", "row3")
+        ts(E(14), PM, 4.0, Op.is_ge, "pmf", "er14")
+        tt(E(15), E(0), E(1), Op.add, "er0 er1", "er15")
+        tt(E(16), E(15), E(14), Op.add, "er15 er14", "er16")
+        ts(C("dg1"), C("idf"), E(16), Op.mult, "idf er16", "dg1")
+        tt(E(17), E(14), E(3), Op.add, "er14 er3", "er17")
+        ts(C("sam", 0, 128), C("idf"), E(17), Op.mult, "idf er17", "sam0")
+        for t in range(RO):
+            ts(C("af%d" % t), C("af%d" % t), E(4 + t), Op.mult, "af%d er%d" % (t, 4 + t), "af%d" % t)
+            tt(C("dgc%d" % t), C("sam", 0, 128), C("af%d" % t), Op.subtract, "sam0 af%d" % t, "dgc%d" % t)
+        ts(C("sam", 128, 256), T.ic[:, 0:128], 0.0, Op.is_equal, "ic", "sam1")
+        ts(C("sam", 256, 384), T.ic[:, 0:128], 1.0, Op.is_equal, "ic", "sam1")
+        tt(C("vrf", 0, 256, p1=32), C("rpf", 256, 512, p1=32), C("sam", 128, 384, p1=32), Op.mult, "rpf sam1", "vrf")
+        tt(C("vr", p1=32), C("vrf", 0, 128, p1=32), C("vrf", 128, 256, p1=32), Op.add, "vrf", "vr")
+        ts(C("vrf", 256, 384, p1=32), C("rpf", 128, 256, p1=32), float(W), Op.mult, "rpf", "vrf2")
+        tt(C("rpc", p1=32), C("vrf", 256, 384, p1=32), C("rpf", 0, 128, p1=32), Op.add, "vrf2 rpf", "rpc")
+
+    def yt_weights():
+        fill(T.wt[:], 0.0, "wt")
+        for c in range(8):
+            ts(T.wt[:, 64 * c + c:64 * c + 64:8], b8, E(11), Op.mult, "blf er11", "wt")
+
+    def disks_out():
+        cp(T.lfu[:], T.lfi[:], "lfi", "lfu")
+        for j in (1, 2, 3):
+            send(T.lfu[:], "lfu", r - j, T["lu%d" % j][:], "rl%d" % j, "ls%d" % (2 * j - 2))
+            send(T.xlh[:], "xlh", r - j, T["xl%d" % j][:], "rx%d" % j, "ls%d" % (2 * j - 1))
+            arrives("rl%d" % j, NE, "lu%d" % j)
+            arrives("rx%d" % j, NE, "xl%d" % j)
+
+    def disk_window(j):
+        cp(T["lw%d" % j][:, 0:M], T["lu%d" % j][:], "lu%d" % j, "lw%d" % j)
+
+    def unpack(j):
+        if j == 0:
+            ts(T.fw[:, 0:2048], T.fdt[:], W - 1, Op.bitwise_and, "fdt", "fw0")
+        else:
+            ts(T.fw[:, 2048:W], T.fdt[:], 12, Op.logical_shift_right, "fdt", "fw1")
+
+    def apply(buf, win):
+        cp(C("lm"), T[buf][:, K:K + 12], buf, "lm")
+        op("v", [lambda: v.tensor_copy(T[win][:].indirect(C("lm")), T[buf][:, 0:K])], buf + " lm", win)
+
+    def dedupe(eq, src, sk, lst, lk, f):
+        for kb in range(11, -1, -1):
+            ts(T[eq][:, kb, 0:K - 16 * kb], src[:, 16 * kb:K], C(lst[0], lst[1] + kb, lst[1] + kb + 1), Op.is_equal, sk + " " + lk, eq)
+        o = K * f
+        fs = [mm(T.psd[:, o:o + K], C("idb"), C("bm"), True, False)]
+        fs += [mm(T.psd[:, o + 16 * kb + 16:o + K], C("blb"), T[eq][:, kb, 16:K - 16 * kb], False, False) for kb in range(10, -1, -1)]
+        fs += [mm(T.psd[:, o + k:o + K:16], C("ltk", 128 * k, 128 * k + 128), T[eq][:, :, k], False, k == 15) for k in range(1, 16)]
+        op("p", fs, "idb bm blb ltk " + eq, "psd")
+
+    def xgather(dst, lst, h):
+        a, b = 16 * H * h, 16 * H * (h + 1)
+        op("v", [lambda: v.tensor_tensor(T[dst][:, a:b], T.xw[:, 0:W].indirect(T[lst][:, H * h:H * h + H]), T.qrep[:, a:b], Op.min)],
+           " ".join((XW, lst, QR)), dst + str(h))
+
+    def pgather(dst, lst, h):
+        a, b = 16 * H * h, 16 * H * (h + 1)
+        act(T[dst][:, a:b], T.pw[:].indirect(T[lst][:, H * h:H * h + H]), PW + " " + lst, dst + str(h))
+
+    def sums(ps, src, w, h, last=False):
+        op("p", [mm(T[ps][0:H, h, i:384:16], T[src][:, 16 * H * h + i:16 * H * (h + 1):16], C(w), False, last and i == 15) for i in range(16)],
+           "%s%d %s" % (src, h, w), "%s%d" % (ps, h))
+
+    def halves(o, l, R, Wt, n, ident):
+        op("p", [mm(o[0:n, H * h:H * h + H], l[0:H, h, 0:n], C(ident, 0, H, p1=H), True, True) for h in (0, 1)], R + " " + ident, Wt)
+
+    def message(t, part):
+        msg = "msg%d" % (t + 1)
+        if part == 0:
+            dedupe("eqt", T.ru[:, 0:K], "ru", ("lis", 0), "lis0", 1)
+            ts(C("pari"), C("ni"), 1, Op.bitwise_and, "ni", "pari")
+            ts(C("w5"), C("pari"), -2.0, Op.mult, "pari", "w5", 1.0, Op.add)
+            tt(C("w6"), C("w5"), C("ni"), Op.add, "w5 ni", "w6")
+            tt(C("w5"), C("w6"), C("dm1"), Op.subtract, "w6 dm1", "w5")
+            return
+        scan(T.sct2[:], T.psd[:, K:2 * K], "psd", "sct2")
+        ts(C("z", 12, 24), T.sct2[:, 15:K:16], 0.0, Op.is_equal, "sct2", "z1")
+        tt(C("dwin"), C("req"), C("z", 12, 24), Op.mult, "req z1", "dwin")
+        tt(C("w6"), C("w5"), C("dwin"), Op.mult, "w5 dwin", "w6")
+        tt(T[msg][:, K:K + 12], C("w6"), C("dm1"), Op.add, "w6 dm1", msg + "l")
+        mk = msg + " " + msg + "l"
+        if t == 0:
+            send(T[msg][:], mk, r - 1, T.up1[:], "ru1", "ls6")
+            send(T[msg][:], mk, r - 2, T.up2[:], "ru2", "ls7")
+            arrives("ru1", NE, "up1")
+            arrives("ru2", NE, "up2")
+        elif t == 1:
+            send(T[msg][:], mk, r - 1, T.up3[:], "ru3", "ls8")
+            arrives("ru3", NE, "up3")
+        send(T[msg][:], mk, r + 1 + t, T["hm%d" % (t + 1)][:], "rh%d" % (t + 1), "ls%d" % (9 + t))
+        arrives("rh%d" % (t + 1), NE, "hm%d" % (t + 1))
+
+    L = lambda n: T[n][0:H, :, :]
+    X = lambda n, i: T[n][0:H, :, 8 * i:8 * i + 8]
+    for t in range(RO):
+        j = t + 1
+        lw, xl, msg = "lw%d" % j, "xl%d" % j, "msg%d" % j
+        for h in (0, 1):
+            pgather("pa", "lc", h)
+        if t == 0:
+            scalar_later()
+            disks_out()
+            weights()
+            for h in (0, 1):
+                xgather("ma", "lc", h)
+        for h in (0, 1):
+            op("p", [mm(T.psk[0:H, h, 0:384], T.ro2[0:1, 0:H], T.row[0:1, 0:384], True, False)], "ro2 row", "psk%d" % h)
+        for h in (0, 1):
+            if t:
+                xgather("ma", "lc", h)
+        if t:
+            ts(T.c16[:], T.cf[:], -2048.0, Op.add, "cf", "c16")
+        else:
+            later()
+        for h in (0, 1):
+            sums("psk", *(("pa", "wp") if t else ("ma", "wm")), h)
+            sums("psk", *(("ma", "wm") if t else ("pa", "wp")), h)
+            op("p", [mm(T.psk[0:H, h, 128:256], T.c16[:, H * h:H * h + H], C("idh"), False, True)], "c16 idh", "psk%d" % h)
+        if t == 0:
+            latest()
+            unpack(0)
+        elif t == 1:
+            disk_window(2)
+            apply("up1", "lw2")
+        else:
+            apply("up2", "lw3")
+            apply("up3", "lw3")
+        act(L("co"), T.psk[0:H, :, 1:256:2], "psk0 psk1", "co")
+        tt(L("t1"), T.psk[0:H, :, 0:256:2], L("co"), Op.min, "psk0 psk1 co", "t1")
+        act(L("sl"), T.psk[0:H, :, 256:384], "psk0 psk1", "sl")
+        tt(L("t2"), T.t1[0:H, :, 0:128:2], T.t1[0:H, :, 1:128:2], Op.min, "t1", "t2")
+        tt(L("t3"), T.t2[0:H, :, 0:64:2], T.t2[0:H, :, 1:64:2], Op.min, "t2", "t3")
+        tt(L("t4"), T.t3[0:H, :, 0:32:2], T.t3[0:H, :, 1:32:2], Op.min, "t3", "t4")
+        ts(X("fi", 1), X("t4", 1), W - 1, Op.bitwise_and, "t4", "fi1")
+        ts(X("fi", 0), X("t4", 0), 2047, Op.bitwise_and, "t4", "fi0")
+        ts(X("fl", 1), X("fi", 1), -2048.0, Op.add, "fi1", "fl1")
+        cp(X("fl", 0), X("fi", 0), "fi0", "fl0")
+        halves(T.psg, T.fl, "fl0 fl1", "psg", 16, "idh")
+        cp(T.gt[0:16, :], T.psg[0:16, 0:K], "psg", "gt")
+        R16 = lambda f: C("rp", 128 * f, 128 * f + 128, p1=16)
+        op("p", [mm(T.psm[:, 0:K], R16(0), T.gt[0:16, :], True, False), mm(T.psm[:, 0:K], C("idb"), C("bm"), False, True)], "rp gt idb bm", "psm")
+        op("p", [mm(T.psu[:, K * f:K * f + K], R16(f), T.gt[0:16, :], True, True) for f in (0, 1)], "rp gt", "psu")
+        op("p", [mm(T.psk[:, 0, 0:K], R16(1), T.gt[0:16, :], True, False), mm(T.psk[:, 0, 0:K], C("idb"), C("bm"), False, True)], "rp gt idb bm", "psk0")
+        if t < 2:
+            disk_window(1 if t == 0 else 3)
+        else:
+            cp(T.lh[:, 0:M], T.lfi[:], "lfi", "lh")
+        scan(T.sct[:], T.psm[:, 0:K], "psm", "sct")
+        ts(C("ni"), T.sct[:, 15:K:16], 1, Op.logical_shift_right, "sct", "ni")
+        cp(C("ln"), C("ni"), "ni", "ln")
+        B = T[lw][:, 0:M]
+        act(T.sq[:, 0:K], B.indirect(C("ln")), lw + " ln", "sq0", AF.Square, bias=4.0)
+        act(T.sq[:, K:2 * K], B.indirect(C("ln")), lw + " ln", "sq1", AF.Square, bias=592.0)
+        op("v", [lambda: v.tensor_copy(T.b16[:], T[lw][:, 0:M].indirect(C("ln")))], lw + " ln", "b16")
+        act(T.at[:], T[xl][:].indirect(C("ln")), xl + " ln", "at")
+        ts(T.ru[:], T.psu[:, 0:2 * K], 2048.0, Op.add, "psu", "ru")
+        for c, (sc, of) in enumerate(((0.125, -2.4375), (0.03125, -10951.484375))):
+            a, b = K * c, K * c + K
+            ts(T.tt[:, a:b], T.sq[:, a:b], sc, Op.mult, "sq%d" % c, "tt%d" % c, of, Op.add)
+            ts(T.cc[:, a:b], T.tt[:, a:b], W - 1, Op.bitwise_and, "tt%d" % c, "cc%d" % c)
+            cp(T["l%d" % (c + 1)][:], T.cc[:, a:b], "cc%d" % c, "l%d" % (c + 1))
+        for h in (0, 1):
+            op("p", [mm(T.psv[0:H, h, :], T.ro2[32:33, 0:H], T.row[32:33, :], True, False),
+                     mm(T.psv[0:H, h, 128:512], T.b16[:, H * h:H * h + H], C("bi"), False, False)], "ro2 row1 b16 bi", "psv%d" % h)
+        for h in (0, 1):
+            pgather("pa", "l1", h)
+            pgather("pb", "l2", h)
+        xgather("ma", "l1", 0)
+        sums("psv", "ma", "wm1", 0)
+        sums("psv", "pa", "wp1", 0)
+        scan(T.sco[:], T.psk[:, 0, 0:K], "psk0", "sco")
+        ts(C("lis", 12, 24), T.sco[:, 15:K:16], 2048.0, Op.add, "sco", "lis1")
+        ts(C("lis", 0, 12), T.sct[:, 15:K:16], 2048.0, Op.add, "sct", "lis0")
+        cp(C("lo"), C("lis", 12, 24), "lis1", "lo")
+        dedupe("eqo", T.ru[:, K:2 * K], "ru", ("lis", 12), "lis1", 0)
+        xgather("mb", "l2", 0)
+        scan(T.scd[:], T.psd[:, 0:K], "psd", "scd")
+        ts(C("ei"), T.sct[:, 15:K:16], 1, Op.bitwise_and, "sct", "ei")
+        ts(C("z", 0, 12), T.scd[:, 15:K:16], 0.0, Op.is_equal, "scd", "z0")
+        tt(C("w1"), C("lis", 12, 24), C("dm4"), Op.subtract, "lis1 dm4", "w1")
+        tt(C("cand"), C("z", 0, 12), C("ei"), Op.mult, "z0 ei", "cand")
+        op("v", [lambda: v.tensor_tensor_scan(C("exb", 1, 13), C("one", 0, 12), C("cand"), 0.0, Op.mult, Op.add)], "one cand", "exb")
+        xgather("ma", "l1", 1)
+        op("p", [mm(T.psk[:, 1, 400:412], C("bt"), C("cand"), True, False), mm(T.psk[:, 1, 400:412], C("blb"), C("exb", 0, 12), False, True)], "bt cand blb exb", "psk1")
+        halves(T.psk[:, 1, :], T.sl, "sl", "psk1", 128, "idf")
+        sums("psv", "mb", "wm2", 0)
+        sums("psv", "pb", "wp2", 0, True)
+        ts(C("rk"), T.psk[:, 1, 400:412], float(CAP), Op.is_le, "psk1", "rk")
+        tt(T.dc[:], T.cc[:, K:2 * K], T.cc[:, 0:K], Op.subtract, "cc0 cc1", "dc")
+        tt(C("req"), C("rk"), C("cand"), Op.mult, "rk cand", "req")
+        tt(C("w2"), C("w1"), C("req"), Op.mult, "w1 req", "w2")
+        ts(C("nrq"), C("req"), -8192.0, Op.mult, "req", "nrq", 8192.0 + 2048.0, Op.add)
+        tt(C("ld"), C("w2"), C("dm4"), Op.add, "w2 dm4", "ld")
+        xgather("mb", "l2", 1)
+        for c, w in (("a", "1"), ("b", "2")):
+            sums("psv", "m" + c, "wm" + w, 1)
+            sums("psv", "p" + c, "wp" + w, 1, c == "b")
+        if t == 0:
+            claim_weights()
+        act(T[msg][:, 0:K], T.psk[:, 1, 0:K], "psk1", msg)
+        act(T.g2[:], T.pw[:].indirect(C("ld")), PW + " ld", "g2")
+        op("p", [mm(T.psk[:, 0, 0:K], C("sa"), T.at[:], True, False), mm(T.psk[:, 0, 0:K], C("dg1"), T.g2[:], False, False),
+                 mm(T.psk[:, 0, 0:K], T.row[96:97, 128 * t:128 * t + 128], T.ro2[96:97, 0:K], False, True)], "sa at dg1 g2 row3 ro2", "psk0")
+        act(T.v2[:], T.psk[:, 0, 0:K], "psk0", "v2")
+        message(t, 0)
+        op("v", [lambda: v.tensor_copy(T.xw[:].indirect(C("ld")), T.at[:])], "ld at", XW)
+        PV = "psv0 psv1"
+        ts(L("r1"), T.psv[0:H, :, 128:256], 0.0, Op.is_equal, PV, "r1", -4096.0, Op.mult)
+        ts(T.psv[0:H, :, 256:384], T.psv[0:H, :, 256:384], 0.0, Op.is_equal, PV, PV, 1024.0, Op.mult)
+        tt(L("u1"), T.psv[0:H, :, 0:128], L("r1"), Op.add, PV + " r1", "u1")
+        tt(L("u2"), T.psv[0:H, :, 256:384], L("u1"), Op.add, PV + " u1", "u2")
+        act(L("ub"), L("u2"), "u2", "ub", AF.Abs)
+        ts(L("pk"), L("u2"), 0.0, Op.is_gt, "u2", "pk")
+        halves(T.psg, T.pk, "pk", "psg", 128, "idb")
+        tt(L("kk"), T.psv[0:H, :, 384:512], L("pk"), Op.add, PV + " pk", "kk")
+        ts(T.psv[0:H, :, 128:256], L("ub"), 512.0, Op.is_gt, "ub", PV, RES, Op.mult)
+        tt(L("k2"), T.psv[0:H, :, 128:256], L("kk"), Op.add, PV + " kk", "k2")
+        tt(L("ka"), T.k2[0:H, :, 0:128:2], T.k2[0:H, :, 1:128:2], Op.min, "k2", "ka")
+        tt(L("kb"), T.ka[0:H, :, 0:64:2], T.ka[0:H, :, 1:64:2], Op.min, "ka", "kb")
+        tt(L("kc"), T.kb[0:H, :, 0:32:2], T.kb[0:H, :, 1:32:2], Op.min, "kb", "kc")
+        tt(L("kd"), T.kc[0:H, :, 0:16:2], T.kc[0:H, :, 1:16:2], Op.min, "kc", "kd")
+        ts(X("t4", 0), L("kd"), 1, Op.logical_shift_right, "kd", "t4", 1023, Op.bitwise_and)
+        ts(X("t4", 1), L("kd"), 1, Op.bitwise_and, "kd", "t4p")
+        ts(X("fg", 0), X("t4", 0), 4.0, Op.add, "t4", "fg")
+        ts(X("fg", 1), X("t4", 0), 592.0, Op.add, "t4", "fg")
+        ts(X("fh", 0), L("kd"), 6, Op.logical_shift_right, "kd", "fh", 31, Op.bitwise_and)
+        tt(T.t3[0:H, :, 0:16], L("fg"), L("fg"), Op.mult, "fg", "t3")
+        ts(X("fh", 1), L("kd"), 1, Op.logical_shift_right, "kd", "fh", 31, Op.bitwise_and)
+        ts(X("fi", 0), X("t3", 0), 0.125, Op.mult, "t3", "fi0", -2.4375, Op.add)
+        ts(X("fi", 1), X("t3", 1), 0.03125, Op.mult, "t3", "fi1", -10951.484375, Op.add)
+        cp(T.fm[0:H, :, 16:32], L("fh"), "fh", "fm1")
+        ts(L("fe"), L("fi"), W - 1, Op.bitwise_and, "fi0 fi1", "fe")
+        ts(X("fm", 1), L("kd"), RES, Op.is_ge, "kd", "fm2")
+        tt(X("t2", 1), X("fe", 1), X("fe", 0), Op.subtract, "fe", "t2")
+        ts(X("t2", 0), X("fe", 0), -2048.0, Op.add, "fe", "t2b")
+        tt(X("t2", 2), X("t2", 1), X("t4", 1), Op.mult, "t2 t4p", "t2c")
+        tt(X("fm", 0), X("t2", 2), X("t2", 0), Op.add, "t2c t2b", "fm0")
+        halves(T.psm, T.fm, "fm0 fm1 fm2", "psm", 32, "idh")
+        tt(T.sp[:], T.psg[:, 0:K], T.dc[:], Op.mult, "psg dc", "sp")
+        cp(T.gu[0:32, :], T.psm[0:32, 0:K], "psm", "gu")
+        op("p", [mm(T.psu[:, 0:K], C("rpc", p1=32), T.gu[0:32, :], True, True)], "rpc gu", "psu")
+        op("p", [mm(T.psg[:, 0:K], C("rpc", p1=32), T.gu[0:32, :], True, False), mm(T.psg[:, 0:K], C("idb"), C("bm"), False, True)], "rpc gu idb bm", "psg")
+        tt(T.sg[:], T.sp[:], T.cc[:, 0:K], Op.add, "sp cc0", "sg")
+        op("v", [lambda: v.tensor_copy(T.pw[:].indirect(C("ld")), T.v2[:])], "ld v2", PW)
+        ts(T.ru2[:], T.psu[:, 0:K], 2048.0, Op.add, "psu", "ru2")
+        scan(T.sco[:], T.psg[:, 0:K], "psg", "sco")
+        tt(C("pls"), C("nrq"), T.sco[:, 15:K:16], Op.add, "nrq sco", "pls")
+        dedupe("eqo", T.ru2, "ru2", ("pls", 0), "pls", 0)
+        ts(C("w3"), C("pls"), float(W), Op.is_lt, "pls", "w3")
+        tt(C("w4"), C("pls"), C("dm4"), Op.subtract, "pls dm4", "w4")
+        if t == 0:
+            unpack(1)
+        op("v", [lambda: v.tensor_copy(T.fw[:].indirect(C("ld")), T.sg[:])], "ld sg", FW)
+        tt(C("w2"), C("w3"), C("w4"), Op.mult, "w3 w4", "w2")
+        op("v", [lambda: v.tensor_tensor(T.qs[:], T.xw[:, 0:W].indirect(C("lo")), T.q[:], Op.add)], XW + " lo q", "qs")
+        op("v", [lambda: v.tensor_copy(T.cf[:], T.fw[:, 0:W].indirect(C("lo")))], FW + " lo", "cf")
+        ts(T.qb[:], T.qs[:], 0.5, Op.mult, "qs", "qb", 127.8125, Op.add)
+        if t < RO - 1:
+            cp(T.lc[:], T.cf[:], "cf", "lc")
+        scan(T.scd[:], T.psd[:, 0:K], "psd", "scd")
+        ts(C("z", 0, 12), T.scd[:, 15:K:16], 0.0, Op.is_equal, "scd", "z0")
+        tt(C("w1"), C("w2"), C("z", 0, 12), Op.mult, "w2 z0", "w1")
+        tt(C("lcl"), C("w1"), C("dm4"), Op.add, "w1 dm4", "lcl")
+        act(T.g1[:], T.pw[:].indirect(C("lcl")), PW + " lcl", "g1")
+        op("p", [mm(T.psm[:, 0:K], C("vr", p1=32), T.gu[0:32, :], True, False),
+                 mm(T.psm[:, 0:K], T.row[0:1, 384:512], T.ro2[0:1, 0:K], False, False),
+                 mm(T.psm[:, 0:K], C("dgc%d" % t), T.g1[:], False, True)], "vr gu row2 ro2 dgc%d g1" % t, "psm")
+        act(T.v1[:], T.psm[:, 0:K], "psm", "v1")
+        if t < RO - 1:
+            for i in range(16):
+                if i % 8 in (1, 4, 6):
+                    act(T.qrep[:, i:16 * K:16], T.qb[:], "qb", "qr%d" % i, AF.Copy, bias=-128.0)
+                else:
+                    ts(T.qrep[:, i:16 * K:16], T.qb[:], -128.0, Op.add, "qb", "qr%d" % i)
+        ts(T.q[:], T.qb[:], -128.0, Op.add, "qb", "q")
+        op("v", [lambda: v.tensor_copy(T.pw[:].indirect(C("lcl")), T.v1[:])], "lcl v1", PW)
+        message(t, 1)
+        if t == 1:
+            yt_weights()
+    dma("d", T.yc[:], T.cf[:], "cf", "yc")
+    dma("d", T.yq[:], T.q[:], "q", "yq")
+    op("p", [mm(T.psv[0:64, 0, :], T.wt[:, 64 * c:64 * c + 64], T.pw[:, 512 * c:512 * c + 512], c == 0, c == 7) for c in range(8)], "wt " + PW, "psv0")
+    for j in (1, 2, 3):
+        apply("hm%d" % j, "lh")
+    act(T.yts[0:64, :], T.psv[0:64, 0, :], "psv0", "yts")
+    dma("d", T.yt[:], T.yts[0:64, :], "yts", "yt")
+    dma("d", T.yl[:], T.lh[:, 0:M], "lh", "yl")
+    finish()

@@ -63,23 +63,27 @@ def tracker(g, T):
             if known[q].get(s2, 0) < v2:
                 known[q][s2] = v2
 
-    def deps(q, comp, R, Wt):
+    def needs(q, comp, R, Wt):
         out = []
         for k in R:
             if k in wr:
-                out.append((wr[k], True))
+                out.append((k, wr[k]))
             if k.startswith("ps"):
-                out += [(x, False) for x in rd.get(k, {}).values()]
+                out += [(k, x) for x in rd.get(k, {}).values()]
         for k in Wt:
             if k in wr:
-                out.append((wr[k], False))
-            out += [(x, False) for x in rd.get(k, {}).values()]
+                out.append((k, wr[k]))
+            out += [(k, x) for x in rd.get(k, {}).values()]
         need = {}
-        for (sem, val, dq), raw in out:
-            if comp and dq == q and q == "p":
+        for k, (sem, val, dq) in out:
+            if comp and dq == q and (q == "p" or k.startswith("ps")):
                 continue
             if need.get(sem, 0) < val:
                 need[sem] = val
+        return need
+
+    def deps(q, comp, R, Wt):
+        need = needs(q, comp, R, Wt)
         for sem in sorted(need, key=lambda s: -len(hist.get((s, need[s]), {}))):
             if known[q].get(sem, 0) < need[sem]:
                 Q[q].wait_ge(T.sem[sem], need[sem])
@@ -92,8 +96,42 @@ def tracker(g, T):
         for k in R:
             rd.setdefault(k, {})[ev[0] if ev[2] is None else q] = ev
 
+    spare, mode = [], {"keep": False, "emit": False}
+
+    def fresh(need):
+        return need.get("qv", 0) == cnt["v"] > 0, any(x != "qv" and known["v"].get(x, 0) < need[x] for x in need)
+
+    def use_spare(need):
+        own, other = fresh(need)
+        n = 2 if other else 1 if own else 0
+        mode["emit"] = True
+        while n and spare:
+            f = spare[0]
+            if any(fresh(needs("v", True, f[1].split(), f[2].split()))):
+                break
+            spare.pop(0)
+            op("v", *f)
+            n -= 1
+        mode["emit"] = False
+
+    def defer(fn):
+        mode["keep"] = True
+        fn()
+        mode["keep"] = False
+
+    def flush():
+        mode["emit"] = True
+        while spare:
+            op("v", *spare.pop(0))
+        mode["emit"] = False
+
     def op(q, fns, R="", Wt=""):
+        if q == "v" and mode["keep"]:
+            spare.append((fns, R, Wt))
+            return
         R, Wt = R.split(), Wt.split()
+        if q == "v" and spare and not mode["emit"]:
+            use_spare(needs(q, True, R, Wt))
         deps(q, True, R, Wt)
         for f in fns[:-1]:
             f()
@@ -131,7 +169,7 @@ def tracker(g, T):
             if known["g"].get(sem, 0) < total[sem]:
                 g.wait_ge(T.sem[sem], total[sem])
                 learn("g", sem, total[sem])
-    return op, dma, before_remote, arrives, finish
+    return op, dma, before_remote, arrives, finish, defer, flush
 
 
 def rank_program(g, core, T, topo):
@@ -139,7 +177,7 @@ def rank_program(g, core, T, topo):
     if r is None:
         return
     v, s, p = g.vector, g.scalar, g.tensor
-    op, dma, before_remote, arrives, finish = tracker(g, T)
+    op, dma, before_remote, arrives, finish, defer, flush = tracker(g, T)
 
     def C(n, a=0, b=None, p0=0, p1=128, st=1):
         bf, o, w = PLACE[n]
@@ -301,9 +339,11 @@ def rank_program(g, core, T, topo):
         for t in range(RO):
             ts(C("af%d" % t), C("af%d" % t), E(4 + t), Op.mult, "af%d er%d" % (t, 4 + t), "af%d" % t)
             tt(C("dgc%d" % t), C("sam", 0, 128), C("af%d" % t), Op.subtract, "sam0 af%d" % t, "dgc%d" % t)
-        ts(C("sam", 128, 256), T.ic[:, 0:128], 0.0, Op.is_equal, "ic", "sam1")
-        ts(C("sam", 256, 384), T.ic[:, 0:128], 1.0, Op.is_equal, "ic", "sam1")
-        tt(C("vrf", 0, 256, p1=32), C("rpf", 256, 512, p1=32), C("sam", 128, 384, p1=32), Op.mult, "rpf sam1", "vrf")
+        ts(C("sam", 128, 256), T.ic[:, 0:128], 1.0, Op.is_equal, "ic", "sam1")
+        ts(C("vrf", 0, 128), T.ic[:, 0:128], 1.0, Op.is_equal, "ic", "vrf", -32.0, Op.mult)
+        ts(C("vrf", 128, 256), T.ic[:, 0:128], 0.0, Op.is_equal, "ic", "vrf1")
+        tt(C("sam", 256, 384), C("vrf", 0, 128), C("vrf", 128, 256), Op.add, "vrf vrf1", "sam2")
+        tt(C("vrf", 0, 256, p1=32), C("rpf", 256, 512, p1=32), C("sam", 128, 384, p1=32), Op.mult, "rpf sam1 sam2", "vrf vrf1")
         tt(C("vr", p1=32), C("vrf", 0, 128, p1=32), C("vrf", 128, 256, p1=32), Op.add, "vrf", "vr")
         ts(C("vrf", 256, 384, p1=32), C("rpf", 128, 256, p1=32), float(W), Op.mult, "rpf", "vrf2")
         tt(C("rpc", p1=32), C("vrf", 256, 384, p1=32), C("rpf", 0, 128, p1=32), Op.add, "vrf2 rpf", "rpc")
@@ -311,7 +351,7 @@ def rank_program(g, core, T, topo):
     def yt_weights():
         fill(T.wt[:], 0.0, "wt")
         for c in range(8):
-            ts(T.wt[:, 64 * c + c:64 * c + 64:8], b8, E(11), Op.mult, "blf er11", "wt")
+            act(T.wt[:, 64 * c + c:64 * c + 64:8], b8, "blf er11 wt", "wt%d" % c, scale=E(11))
 
     def disks_out():
         cp(T.lfu[:], T.lfi[:], "lfi", "lfu")
@@ -334,14 +374,17 @@ def rank_program(g, core, T, topo):
         cp(C("lm"), T[buf][:, K:K + 12], buf, "lm")
         op("v", [lambda: v.tensor_copy(T[win][:].indirect(C("lm")), T[buf][:, 0:K])], buf + " lm", win)
 
-    def dedupe(eq, src, sk, lst, lk, f):
+    EQ = lambda eq: " ".join("%s%d" % (eq, kb) for kb in range(12))
+
+    def same(eq, src, sk, lst, lk):
         for kb in range(11, -1, -1):
-            ts(T[eq][:, kb, 0:K - 16 * kb], src[:, 16 * kb:K], C(lst[0], lst[1] + kb, lst[1] + kb + 1), Op.is_equal, sk + " " + lk, eq)
-        o = K * f
-        fs = [mm(T.psd[:, o:o + K], C("idb"), C("bm"), True, False)]
-        fs += [mm(T.psd[:, o + 16 * kb + 16:o + K], C("blb"), T[eq][:, kb, 16:K - 16 * kb], False, False) for kb in range(10, -1, -1)]
-        fs += [mm(T.psd[:, o + k:o + K:16], C("ltk", 128 * k, 128 * k + 128), T[eq][:, :, k], False, k == 15) for k in range(1, 16)]
-        op("p", fs, "idb bm blb ltk " + eq, "psd")
+            ts(T[eq][:, kb, 0:K - 16 * kb], src[:, 16 * kb:K], C(lst[0], lst[1] + kb, lst[1] + kb + 1), Op.is_equal, sk + " " + lk, eq + str(kb))
+
+    def lower(eq, ps, pk):
+        fs = [mm(ps[:, 0:K], C("idb"), C("bm"), True, False)]
+        fs += [mm(ps[:, 16 * kb + 16:K], C("blb"), T[eq][:, kb, 16:K - 16 * kb], False, False) for kb in range(10, -1, -1)]
+        fs += [mm(ps[:, k:K:16], C("ltk", 128 * k, 128 * k + 128), T[eq][:, :, k], False, k == 15) for k in range(1, 16)]
+        op("p", fs, "idb bm blb ltk " + EQ(eq), pk)
 
     def xgather(dst, lst, h):
         a, b = 16 * H * h, 16 * H * (h + 1)
@@ -362,13 +405,13 @@ def rank_program(g, core, T, topo):
     def message(t, part):
         msg = "msg%d" % (t + 1)
         if part == 0:
-            dedupe("eqt", T.ru[:, 0:K], "ru", ("lis", 0), "lis0", 1)
+            same("eqt", T.ru[:, 0:K], "ru", ("lis", 0), "lis0")
             ts(C("pari"), C("ni"), 1, Op.bitwise_and, "ni", "pari")
             ts(C("w5"), C("pari"), -2.0, Op.mult, "pari", "w5", 1.0, Op.add)
             tt(C("w6"), C("w5"), C("ni"), Op.add, "w5 ni", "w6")
             tt(C("w5"), C("w6"), C("dm1"), Op.subtract, "w6 dm1", "w5")
             return
-        scan(T.sct2[:], T.psd[:, K:2 * K], "psd", "sct2")
+        scan(T.sct2[:], T.psv[:, 0, 0:K], "psv0", "sct2")
         ts(C("z", 12, 24), T.sct2[:, 15:K:16], 0.0, Op.is_equal, "sct2", "z1")
         tt(C("dwin"), C("req"), C("z", 12, 24), Op.mult, "req z1", "dwin")
         tt(C("w6"), C("w5"), C("dwin"), Op.mult, "w5 dwin", "w6")
@@ -390,10 +433,11 @@ def rank_program(g, core, T, topo):
     for t in range(RO):
         j = t + 1
         lw, xl, msg = "lw%d" % j, "xl%d" % j, "msg%d" % j
+        if t == 0:
+            scalar_later()
         for h in (0, 1):
             pgather("pa", "lc", h)
         if t == 0:
-            scalar_later()
             disks_out()
             weights()
             for h in (0, 1):
@@ -413,6 +457,7 @@ def rank_program(g, core, T, topo):
             op("p", [mm(T.psk[0:H, h, 128:256], T.c16[:, H * h:H * h + H], C("idh"), False, True)], "c16 idh", "psk%d" % h)
         if t == 0:
             latest()
+            defer(claim_weights)
             unpack(0)
         elif t == 1:
             disk_window(2)
@@ -450,10 +495,11 @@ def rank_program(g, core, T, topo):
         act(T.at[:], T[xl][:].indirect(C("ln")), xl + " ln", "at")
         ts(T.ru[:], T.psu[:, 0:2 * K], 2048.0, Op.add, "psu", "ru")
         for c, (sc, of) in enumerate(((0.125, -2.4375), (0.03125, -10951.484375))):
-            a, b = K * c, K * c + K
-            ts(T.tt[:, a:b], T.sq[:, a:b], sc, Op.mult, "sq%d" % c, "tt%d" % c, of, Op.add)
-            ts(T.cc[:, a:b], T.tt[:, a:b], W - 1, Op.bitwise_and, "tt%d" % c, "cc%d" % c)
-            cp(T["l%d" % (c + 1)][:], T.cc[:, a:b], "cc%d" % c, "l%d" % (c + 1))
+            ts(T.tt[:, K * c:K * c + K], T.sq[:, K * c:K * c + K], sc, Op.mult, "sq%d" % c, "tt%d" % c, of, Op.add)
+        for c in (0, 1):
+            ts(T.cc[:, K * c:K * c + K], T.tt[:, K * c:K * c + K], W - 1, Op.bitwise_and, "tt%d" % c, "cc%d" % c)
+        for c in (0, 1):
+            cp(T["l%d" % (c + 1)][:], T.cc[:, K * c:K * c + K], "cc%d" % c, "l%d" % (c + 1))
         for h in (0, 1):
             op("p", [mm(T.psv[0:H, h, :], T.ro2[32:33, 0:H], T.row[32:33, :], True, False),
                      mm(T.psv[0:H, h, 128:512], T.b16[:, H * h:H * h + H], C("bi"), False, False)], "ro2 row1 b16 bi", "psv%d" % h)
@@ -467,8 +513,10 @@ def rank_program(g, core, T, topo):
         ts(C("lis", 12, 24), T.sco[:, 15:K:16], 2048.0, Op.add, "sco", "lis1")
         ts(C("lis", 0, 12), T.sct[:, 15:K:16], 2048.0, Op.add, "sct", "lis0")
         cp(C("lo"), C("lis", 12, 24), "lis1", "lo")
-        dedupe("eqo", T.ru[:, K:2 * K], "ru", ("lis", 12), "lis1", 0)
+        same("eqo", T.ru[:, K:2 * K], "ru", ("lis", 12), "lis1")
+        lower("eqo", T.psd, "psd")
         xgather("mb", "l2", 0)
+        defer(lambda: message(t, 0))
         scan(T.scd[:], T.psd[:, 0:K], "psd", "scd")
         ts(C("ei"), T.sct[:, 15:K:16], 1, Op.bitwise_and, "sct", "ei")
         ts(C("z", 0, 12), T.scd[:, 15:K:16], 0.0, Op.is_equal, "scd", "z0")
@@ -491,46 +539,46 @@ def rank_program(g, core, T, topo):
             sums("psv", "m" + c, "wm" + w, 1)
             sums("psv", "p" + c, "wp" + w, 1, c == "b")
         if t == 0:
-            claim_weights()
+            flush()
         act(T[msg][:, 0:K], T.psk[:, 1, 0:K], "psk1", msg)
         act(T.g2[:], T.pw[:].indirect(C("ld")), PW + " ld", "g2")
         op("p", [mm(T.psk[:, 0, 0:K], C("sa"), T.at[:], True, False), mm(T.psk[:, 0, 0:K], C("dg1"), T.g2[:], False, False),
                  mm(T.psk[:, 0, 0:K], T.row[96:97, 128 * t:128 * t + 128], T.ro2[96:97, 0:K], False, True)], "sa at dg1 g2 row3 ro2", "psk0")
         act(T.v2[:], T.psk[:, 0, 0:K], "psk0", "v2")
-        message(t, 0)
         op("v", [lambda: v.tensor_copy(T.xw[:].indirect(C("ld")), T.at[:])], "ld at", XW)
         PV = "psv0 psv1"
         ts(L("r1"), T.psv[0:H, :, 128:256], 0.0, Op.is_equal, PV, "r1", -4096.0, Op.mult)
-        ts(T.psv[0:H, :, 256:384], T.psv[0:H, :, 256:384], 0.0, Op.is_equal, PV, PV, 1024.0, Op.mult)
+        ts(T.psv[0:H, :, 256:384], T.psv[0:H, :, 256:384], 0.0, Op.is_equal, PV, PV + " r2", 1024.0, Op.mult)
         tt(L("u1"), T.psv[0:H, :, 0:128], L("r1"), Op.add, PV + " r1", "u1")
-        tt(L("u2"), T.psv[0:H, :, 256:384], L("u1"), Op.add, PV + " u1", "u2")
+        tt(L("u2"), T.psv[0:H, :, 256:384], L("u1"), Op.add, PV + " u1 r2", "u2")
         act(L("ub"), L("u2"), "u2", "ub", AF.Abs)
         ts(L("pk"), L("u2"), 0.0, Op.is_gt, "u2", "pk")
         halves(T.psg, T.pk, "pk", "psg", 128, "idb")
         tt(L("kk"), T.psv[0:H, :, 384:512], L("pk"), Op.add, PV + " pk", "kk")
-        ts(T.psv[0:H, :, 128:256], L("ub"), 512.0, Op.is_gt, "ub", PV, RES, Op.mult)
-        tt(L("k2"), T.psv[0:H, :, 128:256], L("kk"), Op.add, PV + " kk", "k2")
+        ts(T.psv[0:H, :, 128:256], L("ub"), 512.0, Op.is_gt, "ub r1", PV + " r3", RES, Op.mult)
+        tt(L("k2"), T.psv[0:H, :, 128:256], L("kk"), Op.add, PV + " kk r3", "k2")
         tt(L("ka"), T.k2[0:H, :, 0:128:2], T.k2[0:H, :, 1:128:2], Op.min, "k2", "ka")
         tt(L("kb"), T.ka[0:H, :, 0:64:2], T.ka[0:H, :, 1:64:2], Op.min, "ka", "kb")
         tt(L("kc"), T.kb[0:H, :, 0:32:2], T.kb[0:H, :, 1:32:2], Op.min, "kb", "kc")
         tt(L("kd"), T.kc[0:H, :, 0:16:2], T.kc[0:H, :, 1:16:2], Op.min, "kc", "kd")
         ts(X("t4", 0), L("kd"), 1, Op.logical_shift_right, "kd", "t4", 1023, Op.bitwise_and)
-        ts(X("t4", 1), L("kd"), 1, Op.bitwise_and, "kd", "t4p")
-        ts(X("fg", 0), X("t4", 0), 4.0, Op.add, "t4", "fg")
-        ts(X("fg", 1), X("t4", 0), 592.0, Op.add, "t4", "fg")
-        ts(X("fh", 0), L("kd"), 6, Op.logical_shift_right, "kd", "fh", 31, Op.bitwise_and)
-        tt(T.t3[0:H, :, 0:16], L("fg"), L("fg"), Op.mult, "fg", "t3")
-        ts(X("fh", 1), L("kd"), 1, Op.logical_shift_right, "kd", "fh", 31, Op.bitwise_and)
+        ts(X("t4", 1), L("kd"), 6, Op.logical_shift_right, "kd", "t4p", 31, Op.bitwise_and)
+        ts(X("fg", 0), X("t4", 0), 4.0, Op.add, "t4", "fg0")
+        ts(X("fg", 1), X("t4", 0), 592.0, Op.add, "t4", "fg1")
+        ts(X("fh", 0), L("kd"), 1, Op.bitwise_and, "kd", "fh")
+        tt(T.t3[0:H, :, 0:16], L("fg"), L("fg"), Op.mult, "fg0 fg1", "t3")
+        cp(T.fm[0:H, :, 16:32], L("t4"), "t4 t4p", "fm1")
         ts(X("fi", 0), X("t3", 0), 0.125, Op.mult, "t3", "fi0", -2.4375, Op.add)
         ts(X("fi", 1), X("t3", 1), 0.03125, Op.mult, "t3", "fi1", -10951.484375, Op.add)
-        cp(T.fm[0:H, :, 16:32], L("fh"), "fh", "fm1")
-        ts(L("fe"), L("fi"), W - 1, Op.bitwise_and, "fi0 fi1", "fe")
         ts(X("fm", 1), L("kd"), RES, Op.is_ge, "kd", "fm2")
+        ts(L("fe"), L("fi"), W - 1, Op.bitwise_and, "fi0 fi1", "fe")
         tt(X("t2", 1), X("fe", 1), X("fe", 0), Op.subtract, "fe", "t2")
         ts(X("t2", 0), X("fe", 0), -2048.0, Op.add, "fe", "t2b")
-        tt(X("t2", 2), X("t2", 1), X("t4", 1), Op.mult, "t2 t4p", "t2c")
+        tt(X("t2", 2), X("t2", 1), X("fh", 0), Op.mult, "t2 fh", "t2c")
         tt(X("fm", 0), X("t2", 2), X("t2", 0), Op.add, "t2c t2b", "fm0")
+        flush()
         halves(T.psm, T.fm, "fm0 fm1 fm2", "psm", 32, "idh")
+        lower("eqt", T.psv[:, 0, :], "psv0")
         tt(T.sp[:], T.psg[:, 0:K], T.dc[:], Op.mult, "psg dc", "sp")
         cp(T.gu[0:32, :], T.psm[0:32, 0:K], "psm", "gu")
         op("p", [mm(T.psu[:, 0:K], C("rpc", p1=32), T.gu[0:32, :], True, True)], "rpc gu", "psu")
@@ -540,7 +588,8 @@ def rank_program(g, core, T, topo):
         ts(T.ru2[:], T.psu[:, 0:K], 2048.0, Op.add, "psu", "ru2")
         scan(T.sco[:], T.psg[:, 0:K], "psg", "sco")
         tt(C("pls"), C("nrq"), T.sco[:, 15:K:16], Op.add, "nrq sco", "pls")
-        dedupe("eqo", T.ru2, "ru2", ("pls", 0), "pls", 0)
+        same("eqo", T.ru2, "ru2", ("pls", 0), "pls")
+        lower("eqo", T.psd, "psd")
         ts(C("w3"), C("pls"), float(W), Op.is_lt, "pls", "w3")
         tt(C("w4"), C("pls"), C("dm4"), Op.subtract, "pls dm4", "w4")
         if t == 0:
@@ -552,6 +601,12 @@ def rank_program(g, core, T, topo):
         ts(T.qb[:], T.qs[:], 0.5, Op.mult, "qs", "qb", 127.8125, Op.add)
         if t < RO - 1:
             cp(T.lc[:], T.cf[:], "cf", "lc")
+            for i in range(16):
+                if i % 8 in (1, 4, 6):
+                    act(T.qrep[:, i:16 * K:16], T.qb[:], "qb", "qr%d" % i, AF.Copy, bias=-128.0)
+                else:
+                    defer(lambda: ts(T.qrep[:, i:16 * K:16], T.qb[:], -128.0, Op.add, "qb", "qr%d" % i))
+        defer(lambda: ts(T.q[:], T.qb[:], -128.0, Op.add, "qb", "q"))
         scan(T.scd[:], T.psd[:, 0:K], "psd", "scd")
         ts(C("z", 0, 12), T.scd[:, 15:K:16], 0.0, Op.is_equal, "scd", "z0")
         tt(C("w1"), C("w2"), C("z", 0, 12), Op.mult, "w2 z0", "w1")
@@ -561,20 +616,14 @@ def rank_program(g, core, T, topo):
                  mm(T.psm[:, 0:K], T.row[0:1, 384:512], T.ro2[0:1, 0:K], False, False),
                  mm(T.psm[:, 0:K], C("dgc%d" % t), T.g1[:], False, True)], "vr gu row2 ro2 dgc%d g1" % t, "psm")
         act(T.v1[:], T.psm[:, 0:K], "psm", "v1")
-        if t < RO - 1:
-            for i in range(16):
-                if i % 8 in (1, 4, 6):
-                    act(T.qrep[:, i:16 * K:16], T.qb[:], "qb", "qr%d" % i, AF.Copy, bias=-128.0)
-                else:
-                    ts(T.qrep[:, i:16 * K:16], T.qb[:], -128.0, Op.add, "qb", "qr%d" % i)
-        ts(T.q[:], T.qb[:], -128.0, Op.add, "qb", "q")
+        flush()
         op("v", [lambda: v.tensor_copy(T.pw[:].indirect(C("lcl")), T.v1[:])], "lcl v1", PW)
         message(t, 1)
         if t == 1:
             yt_weights()
     dma("d", T.yc[:], T.cf[:], "cf", "yc")
     dma("d", T.yq[:], T.q[:], "q", "yq")
-    op("p", [mm(T.psv[0:64, 0, :], T.wt[:, 64 * c:64 * c + 64], T.pw[:, 512 * c:512 * c + 512], c == 0, c == 7) for c in range(8)], "wt " + PW, "psv0")
+    op("p", [mm(T.psv[0:64, 0, :], T.wt[:, 64 * c:64 * c + 64], T.pw[:, 512 * c:512 * c + 512], c == 0, c == 7) for c in range(8)], " ".join("wt%d" % c for c in range(8)) + " " + PW, "psv0")
     for j in (1, 2, 3):
         apply("hm%d" % j, "lh")
     act(T.yts[0:64, :], T.psv[0:64, 0, :], "psv0", "yts")

@@ -5,6 +5,9 @@ H = 96
 BIG = 65536.0
 RES = 1048576.0
 NE = 8
+WAKE, SLACK = 0.3, 0.1
+VCOST = {"ma": 1.7, "mb": 1.7, "xw": 0.6, "pw": 0.6, "fw": 0.7, "lw": 0.7, "lh": 0.7, "lfu": 0.85, "pcs": 0.64, "sq": 0.2, "cf": 0.25, "qs": 0.25, "eqo": 0.07, "eqt": 0.07, "cc": 0.12, "dc": 0.32, "sp": 0.16, "sg": 0.32, "u": 0.11}
+SCOST = {"pa": 1.7, "pb": 1.7, "pw": 0.43, "g": 0.28, "at": 0.15, "wt": 0.06, "ltk": 0.11, "wm": 0.06, "wp": 0.06}
 
 _S = "sbuf"
 F32, B16, I32, U16, H16 = "float32", "bfloat16", "int32", "uint16", "float16"
@@ -14,7 +17,7 @@ PACK = {
     "tl": (U16, (("ln", 12), ("lo", 12), ("ld", 12), ("lcl", 12), ("lm", 12))),
     "ti": (I32, (("ni", 12), ("ei", 12), ("pari", 12), ("dmi", 12), ("pmi", 4))),
     "tb": (B16, (("wm", 24), ("wp", 24), ("wm1", 24), ("wm2", 24), ("wp1", 24), ("wp2", 24), ("cand", 12), ("exb", 16))),
-    "cb": (B16, (("idb", 128), ("blb", 128), ("bt", 128), ("dg1", 128), ("sa", 128), ("dgc0", 128), ("dgc1", 128), ("dgc2", 128), ("bm", K), ("ltk", 2048))),
+    "cb": (B16, (("idb", 128), ("blb", 128), ("bt", 128), ("dg1", 128), ("sa", 128), ("dgc0", 128), ("dgc1", 128), ("dgc2", 128), ("bm", K), ("ltk", 2048), ("pb16", 128), ("nb16", 128))),
     "cff": (F32, (("one", 512), ("idf", 128), ("blf", 128), ("btf", 128), ("af0", 128), ("af1", 128), ("af2", 128), ("sam", 384), ("rpf", 512), ("vrf", 384))),
     "chh": (H16, (("rp", 512), ("rpc", 128), ("vr", 128), ("bi", 384), ("idh", 128))),
 }
@@ -27,8 +30,8 @@ for _b in PACK:
     SCRATCH[_b] = (_S, [128, _o], PACK[_b][0])
 for _d, _l in (
     (B16, (("xw", W + K), ("pw", W + K), ("pcs", 768), ("xlh", M), ("q", K), ("qb", K), ("qrep", 16 * K), ("ma", 16 * K), ("mb", 16 * K), ("pa", 16 * K), ("pb", 16 * K),
-           ("at", K), ("g1", K), ("v1", K), ("g2", K), ("v2", K), ("row", 512), ("ro2", 512), ("wt", 512), ("xl1", M), ("xl2", M), ("xl3", M))),
-    (I32, (("fw", W + K), ("fdt", 2048), ("tgs", 256), ("pci", 768), ("lfi", M), ("cxi", K), ("sct", K), ("sco", K), ("tt", 2 * K), ("cc", 2 * K), ("dc", K), ("sg", K), ("ia", K), ("ic", 512))),
+           ("at", K), ("g1", K), ("v1", K), ("g2", K), ("v2", K), ("row", 512), ("ro2", 512), ("wt", 512), ("xl1", M), ("xl2", M), ("xl3", M), ("xp1", 512), ("xp2", 512), ("xp3", 512), ("xlp", 512), ("xt", 512))),
+    (I32, (("fw", W + K), ("fdt", 2048), ("tgs", 256), ("pci", 768), ("lfi", M), ("cxi", K), ("sct", K), ("sco", K), ("scl", K), ("tt", 2 * K), ("cc", 2 * K), ("dc", K), ("sg", K), ("ia", K), ("ic", 512))),
     (U16, (("lfu", M), ("lc", K), ("ru", 2 * K), ("ru2", K), ("l1", K), ("l2", K), ("lu1", M), ("lu2", M), ("lu3", M))),
     (F32, (("lh", M + K), ("qs", K), ("cf", K), ("scd", K), ("sct2", K), ("sq", 2 * K), ("sp", K), ("yts", 512), ("s0", K), ("lw1", M), ("lw2", M + K), ("lw3", M + K),
            ("msg1", K + 12), ("msg2", K + 12), ("msg3", K + 12), ("up1", K + 12), ("up2", K + 12), ("up3", K + 12), ("hm1", K + 12), ("hm2", K + 12), ("hm3", K + 12))),
@@ -37,7 +40,7 @@ for _d, _l in (
     for _n, _w in _l:
         SCRATCH[_n] = (_S, [128, _w], _d)
 for _n, _w, _d in (("co", 128, F32), ("t1", 128, F32), ("t2", 64, F32), ("t3", 32, F32), ("t4", 16, I32), ("fi", 16, I32), ("fl", 16, H16), ("sl", 128, F32), ("r1", 128, F32), ("r2", 128, F32), ("u1", 128, F32),
-                   ("u2", 128, F32), ("ub", 128, F32), ("pk", 128, B16), ("kk", 128, F32), ("k2", 128, F32), ("ka", 64, F32), ("kb", 32, F32), ("kc", 16, F32), ("kd", 8, I32), ("fe", 16, I32), ("fg", 16, F32), ("fh", 16, I32), ("fm", 32, H16)):
+                   ("u2", 128, F32), ("ub", 128, F32), ("pk", 128, B16), ("kk", 128, F32), ("k2", 128, F32), ("ka", 64, F32), ("kb", 32, F32), ("kc", 16, F32), ("kd", 8, I32), ("fe", 16, I32), ("fg", 16, F32), ("fh", 16, I32), ("fm", 32, H16), ("t5", 16, F32), ("t6", 32, F32), ("t7", 16, I32), ("fj", 16, I32)):
     SCRATCH[_n] = (_S, [128, 2, _w], _d)
 SCRATCH["eqo"] = (_S, [128, 12, K], B16)
 SCRATCH["eqt"] = (_S, [128, 12, K], B16)
@@ -45,7 +48,7 @@ for _n in ("psk", "psv"):
     SCRATCH[_n] = ("psum", [128, 2, 512], F32)
 for _n in ("psm", "psu", "psd", "psg"):
     SCRATCH[_n] = ("psum", [128, 512], F32)
-SEMAPHORES = ["qv", "qs", "qp", "qg"] + ["ld%d" % j for j in range(20)] + ["ls%d" % j for j in range(12)]
+SEMAPHORES = ["qv", "qs", "qp", "qg"] + ["ld%d" % j for j in range(20)] + ["ls%d" % j for j in range(16)]
 SEMAPHORES += ["%s%d" % (a, j) for a in ("rl", "rx", "ru", "rh") for j in (1, 2, 3)]
 
 
@@ -96,42 +99,8 @@ def tracker(g, T):
         for k in R:
             rd.setdefault(k, {})[ev[0] if ev[2] is None else q] = ev
 
-    spare, mode = [], {"keep": False, "emit": False}
-
-    def fresh(need):
-        return need.get("qv", 0) == cnt["v"] > 0, any(x != "qv" and known["v"].get(x, 0) < need[x] for x in need)
-
-    def use_spare(need):
-        own, other = fresh(need)
-        n = 2 if other else 1 if own else 0
-        mode["emit"] = True
-        while n and spare:
-            f = spare[0]
-            if any(fresh(needs("v", True, f[1].split(), f[2].split()))):
-                break
-            spare.pop(0)
-            op("v", *f)
-            n -= 1
-        mode["emit"] = False
-
-    def defer(fn):
-        mode["keep"] = True
-        fn()
-        mode["keep"] = False
-
-    def flush():
-        mode["emit"] = True
-        while spare:
-            op("v", *spare.pop(0))
-        mode["emit"] = False
-
-    def op(q, fns, R="", Wt=""):
-        if q == "v" and mode["keep"]:
-            spare.append((fns, R, Wt))
-            return
+    def op_(q, fns, R, Wt):
         R, Wt = R.split(), Wt.split()
-        if q == "v" and spare and not mode["emit"]:
-            use_spare(needs(q, True, R, Wt))
         deps(q, True, R, Wt)
         for f in fns[:-1]:
             f()
@@ -144,7 +113,7 @@ def tracker(g, T):
             hist[(sem, cnt[q])][sem] = cnt[q] - 1
         note((sem, cnt[q], q), q, R, Wt)
 
-    def dma(q, out, in_, R="", Wt=""):
+    def dma_(q, out, in_, R, Wt):
         R, Wt = R.split(), Wt.split()
         deps(q, False, R, Wt)
         sem = "ld%d" % nd[0]
@@ -154,22 +123,116 @@ def tracker(g, T):
         hist[(sem, 16)] = dict(known[q])
         note((sem, 16, None), q, R, Wt)
 
-    def before_remote(R, local, n):
+    def send_(call, R, local, n):
         deps("g", False, R.split(), [])
+        call()
         total[local] = n
         note((local, n, None), "g", R.split(), [])
 
-    def arrives(sem, n, key):
+    def arrives_(sem, n, key):
         total[sem] = n
         wr[key] = (sem, n, None)
         rd[key] = {}
 
+    nodes = []
+
+    def op(q, fns, R="", Wt=""):
+        nodes.append((q, R.split(), Wt.split(), lambda: op_(q, fns, R, Wt), len(fns), 0.0, -1))
+
+    def dma(q, out, in_, R="", Wt="", lat=2.2):
+        nodes.append((q, R.split(), Wt.split(), lambda: dma_(q, out, in_, R, Wt), 0, lat, -1))
+
+    def send(call, R, local, n):
+        nodes.append(("g", R.split(), [], lambda: send_(call, R, local, n), 0, 0.0, -1))
+
+    def arrives(sem, n, key, lat):
+        nodes.append(("a", [], [key], lambda: arrives_(sem, n, key), 0, lat, len(nodes) - 1))
+
+    def cost(q, W1, n):
+        if q == "p":
+            return 0.05 * n
+        if n == 0:
+            return 0.3 if q == "g" else 0.1
+        if q == "g":
+            return 0.6
+        return (SCOST if q == "s" else VCOST).get(W1, 0.2 if q == "s" else 0.09)
+
     def finish():
+        nn = len(nodes)
+        dep = [set() for _ in nodes]
+        w, rds, ps = {}, {}, {}
+        for x, (q, R, Wt, f, n, lat, after) in enumerate(nodes):
+            if after >= 0:
+                dep[x].add(after)
+            for k in sorted(set(R + Wt)):
+                if k.startswith("ps"):
+                    cur = ps.setdefault(k, [q, [], []])
+                    if cur[0] == q:
+                        dep[x].update(cur[2])
+                        if q == "p" and cur[1]:
+                            dep[x].add(cur[1][-1])
+                        cur[1].append(x)
+                    else:
+                        dep[x].update(cur[1])
+                        ps[k] = [q, [x], cur[1]]
+                    continue
+                if k in w:
+                    dep[x].add(w[k])
+                if k in Wt:
+                    dep[x].update(rds.get(k, []))
+            for k in Wt:
+                w[k], rds[k] = x, []
+            for k in R:
+                if k not in Wt:
+                    rds.setdefault(k, []).append(x)
+            dep[x].discard(x)
+        succ = [[] for _ in nodes]
+        for x in range(nn):
+            for d in dep[x]:
+                succ[d].append(x)
+        cs = [0.0 if nd_[0] == "a" else cost(nd_[0], (nd_[2] + nd_[1] + [""])[0].rstrip("0123456789"), nd_[4]) for nd_ in nodes]
+        pr = [0.0] * nn
+        for x in range(nn - 1, -1, -1):
+            pr[x] = cs[x] + nodes[x][5] + max([pr[y] + WAKE for y in succ[x]] + [0.0])
+        left = [len(d) for d in dep]
+        ready = {q: [] for q in "vspgda"}
+        fin, qt = [0.0] * nn, {q: 0.0 for q in "vspgda"}
+        early = [0.0] * nn
+        for x in range(nn):
+            if not left[x]:
+                ready[nodes[x][0]].append(x)
+        for _ in range(nn):
+            best = None
+            for q in "avspgd":
+                if not ready[q]:
+                    continue
+                st = {}
+                for x in ready[q]:
+                    e = early[x]
+                    st[x] = e if q == "a" else (e + WAKE if e > qt[q] - 0.001 else qt[q])
+                lo = min(st.values())
+                if q in "gd":
+                    x = min(ready[q])
+                else:
+                    x = max((y for y in st if st[y] <= lo + SLACK), key=lambda y: (pr[y], -y))
+                if best is None or st[x] < best[0]:
+                    best = (st[x], q, x)
+            t0, q, x = best
+            ready[q].remove(x)
+            e = t0 + cs[x]
+            qt[q] = e
+            fin[x] = e + nodes[x][5]
+            nodes[x][3]()
+            for y in succ[x]:
+                left[y] -= 1
+                early[y] = max(early[y], fin[x])
+                if not left[y]:
+                    ready[nodes[y][0]].append(y)
         for sem in total:
             if known["g"].get(sem, 0) < total[sem]:
                 g.wait_ge(T.sem[sem], total[sem])
                 learn("g", sem, total[sem])
-    return op, dma, before_remote, arrives, finish, defer, flush
+    return op, dma, send, arrives, finish
 
 
 def rank_program(g, core, T, topo):
@@ -177,7 +240,7 @@ def rank_program(g, core, T, topo):
     if r is None:
         return
     v, s, p = g.vector, g.scalar, g.tensor
-    op, dma, before_remote, arrives, finish, defer, flush = tracker(g, T)
+    op, dma, put, arrives, finish = tracker(g, T)
 
     def C(n, a=0, b=None, p0=0, p1=128, st=1):
         bf, o, w = PLACE[n]
@@ -204,29 +267,29 @@ def rank_program(g, core, T, topo):
     def mm(o, l, x, st, sp):
         return lambda: p.matmul(o, l, x, st, sp)
 
-    def scan(o, d, R, Wt):
-        op("v", [lambda: v.tensor_tensor_scan(o, T.s0[:], d, 0.0, Op.add, Op.min)], R + " s0", Wt)
+    def scan(o, d, R, Wt, n=K):
+        op("v", [lambda: v.tensor_tensor_scan(o, T.s0[:, 0:n], d, 0.0, Op.add, Op.min)], R + " s0", Wt)
 
-    def send(src, key, dst_rank, dst, sem, local):
+    def send(src, key, dst_rank, dst, sem, local, bulk=False):
         dst_core = T.cores[dst_rank % N]
         rid, pid = topo.addr(dst_core)[0:2]
-        eng = topo.engines(core, dst_core)[0:NE]
-        before_remote(key, local, len(eng))
-        g.remote_dma(dst, src, T.sem[sem], T.sem[local], pid, rid, sum(1 << e for e in eng))
+        eng = topo.engines(core, dst_core)
+        eng = eng[-NE:] if bulk else eng[0:NE]
+        put(lambda: g.remote_dma(dst, src, T.sem[sem], T.sem[local], pid, rid, sum(1 << e for e in eng)), key, local, len(eng))
 
     PWI = " ".join("pw%d" % c for c in range(8))
     PW = PWI + " pwr0 pwr1 pwr2 pwd"
     XW = "xw0 xw1"
     FW = "fw0 fw1"
     QR = " ".join("qr%d" % i for i in range(16))
-    dma("d", T.xw[:, 0:2048], T.xr[:, 0:2048], "", "xw0")
-    dma("s", T.tgs[:], T.tg[:], "", "tgs")
-    dma("d", T.xw[:, 2048:W], T.xr[:, 2048:W], "", "xw1")
-    dma("s", T.cxi[:], T.cx[:], "", "cxi")
-    dma("s", T.q[:], T.qx[:], "", "q")
-    dma("s", T.lfi[:], T.lf[:], "", "lfi")
-    dma("d", T.xlh[:], T.xl[:], "", "xlh")
-    dma("d", T.fdt[:], T.fd[:], "", "fdt")
+    dma("s", T.tgs[:], T.tg[:], "", "tgs", 2.7)
+    dma("d", T.xw[:, 0:2048], T.xr[:, 0:2048], "", "xw0", 5.0)
+    dma("s", T.cxi[:], T.cx[:], "", "cxi", 5.0)
+    dma("s", T.q[:], T.qx[:], "", "q", 5.0)
+    dma("d", T.xw[:, 2048:W], T.xr[:, 2048:W], "", "xw1", 7.5)
+    dma("s", T.lfi[:], T.lf[:], "", "lfi", 9.0)
+    dma("d", T.xlh[:], T.xl[:], "", "xlh", 10.5)
+    dma("d", T.fdt[:], T.fd[:], "", "fdt", 16.0)
     fill(C("one"), 1.0, "one")
     gop = lambda f, R, Wt: op("g", [f], R, Wt)
     gop(lambda: g.iota(C("pmi", 0, 1), [[0, 1]], 0, 1), "", "pmi")
@@ -290,7 +353,7 @@ def rank_program(g, core, T, topo):
         else:
             act(T.pw[:, 512 * c:512 * c + 512], ap, bk, "pw%d" % c)
     for j in range(3):
-        dma("d", T.pw[j:128:16, 0:W], T.pcs[:, 256 * j:256 * j + 256], "pcs " + PWI, "pwr%d" % j)
+        dma("d", T.pw[j:128:16, 0:W], T.pcs[:, 256 * j:256 * j + 256], "pcs " + PWI, "pwr%d" % j, 3.5)
 
     def weights():
         fill(T.row[:], 0.0, "row")
@@ -355,11 +418,32 @@ def rank_program(g, core, T, topo):
 
     def disks_out():
         cp(T.lfu[:], T.lfi[:], "lfi", "lfu")
+        chip = lambda x: topo.chip(T.cores[x % N])
+
+        def handed(src, j):
+            return j > 1 and chip(src - j) == chip(src - j + 1) != chip(src)
+        act(C("pb16"), C("idf"), "idf", "pb16", scale=16.0)
+        act(C("nb16"), C("idf"), "idf", "nb16", scale=-16.0)
+        op("p", [mm(T.psg[:], C("idb"), T.xlh[:, 0:512], True, False), mm(T.psg[:], C("pb16"), T.xlh[:, 512:M], False, True)], "idb pb16 xlh", "psg")
+        act(T.xlp[:], T.psg[:], "psg", "xlp")
         for j in (1, 2, 3):
-            send(T.lfu[:], "lfu", r - j, T["lu%d" % j][:], "rl%d" % j, "ls%d" % (2 * j - 2))
-            send(T.xlh[:], "xlh", r - j, T["xl%d" % j][:], "rx%d" % j, "ls%d" % (2 * j - 1))
-            arrives("rl%d" % j, NE, "lu%d" % j)
-            arrives("rx%d" % j, NE, "xl%d" % j)
+            if not handed(r, j):
+                send(T.lfu[:], "lfu", r - j, T["lu%d" % j][:], "rl%d" % j, "ls%d" % (2 * j - 2), True)
+            arrives("rl%d" % j, NE, "lu%d" % j, (9.0, 30.0, 40.0)[j - 1])
+            if not handed(r, j):
+                send(T.xlp[:], "xlp", r - j, T["xp%d" % j][:], "rx%d" % j, "ls%d" % (2 * j - 1), True)
+            arrives("rx%d" % j, NE, "xp%d" % j, (13.0, 35.0, 45.0)[j - 1])
+        for i in (1, 2):
+            if handed(r + i, i + 1):
+                send(T["lu%d" % i][:], "lu%d" % i, r - 1, T["lu%d" % (i + 1)][:], "rl%d" % (i + 1), "ls%d" % (10 + 2 * i), True)
+                send(T["xp%d" % i][:], "xp%d" % i, r - 1, T["xp%d" % (i + 1)][:], "rx%d" % (i + 1), "ls%d" % (11 + 2 * i), True)
+
+    def features(j):
+        x, xl = T["xp%d" % j], T["xl%d" % j]
+        act(T.xt[:], x[:], "xp%d" % j, "xt", AF.Copy, scale=0.0625, bias=144.0 - 0.46875)
+        act(xl[:, 512:M], T.xt[:], "xt", "xh%d" % j, AF.Copy, bias=-144.0)
+        op("p", [mm(T.psg[:], C("idb"), x[:], True, False), mm(T.psg[:], C("nb16"), xl[:, 512:M], False, True)], "idb nb16 xp%d xh%d" % (j, j), "psg")
+        act(xl[:, 0:512], T.psg[:], "psg", "xl%d" % j)
 
     def disk_window(j):
         cp(T["lw%d" % j][:, 0:M], T["lu%d" % j][:], "lu%d" % j, "lw%d" % j)
@@ -372,7 +456,7 @@ def rank_program(g, core, T, topo):
 
     def apply(buf, win):
         cp(C("lm"), T[buf][:, K:K + 12], buf, "lm")
-        op("v", [lambda: v.tensor_copy(T[win][:].indirect(C("lm")), T[buf][:, 0:K])], buf + " lm", win)
+        cp(T[win][:].indirect(C("lm")), T[buf][:, 0:K], buf + " lm", win)
 
     EQ = lambda eq: " ".join("%s%d" % (eq, kb) for kb in range(12))
 
@@ -386,14 +470,12 @@ def rank_program(g, core, T, topo):
         fs += [mm(ps[:, k:K:16], C("ltk", 128 * k, 128 * k + 128), T[eq][:, :, k], False, k == 15) for k in range(1, 16)]
         op("p", fs, "idb bm blb ltk " + EQ(eq), pk)
 
-    def xgather(dst, lst, h):
-        a, b = 16 * H * h, 16 * H * (h + 1)
-        op("v", [lambda: v.tensor_tensor(T[dst][:, a:b], T.xw[:, 0:W].indirect(T[lst][:, H * h:H * h + H]), T.qrep[:, a:b], Op.min)],
-           " ".join((XW, lst, QR)), dst + str(h))
+    def xgather(dst, lst, lk, h):
+        a, b = H * h, H * h + H
+        tt(T[dst][:, 16 * a:16 * b], T.xw[:, 0:W].indirect(T[lst][:, a:b]), T.qrep[:, 16 * a:16 * b], Op.min, " ".join((XW, lk, QR)), dst + str(h))
 
-    def pgather(dst, lst, h):
-        a, b = 16 * H * h, 16 * H * (h + 1)
-        act(T[dst][:, a:b], T.pw[:].indirect(T[lst][:, H * h:H * h + H]), PW + " " + lst, dst + str(h))
+    def pgather(dst, lst, lk, h):
+        act(T[dst][:, 16 * H * h:16 * H * (h + 1)], T.pw[:].indirect(T[lst][:, H * h:H * h + H]), PW + " " + lk, dst + str(h))
 
     def sums(ps, src, w, h, last=False):
         op("p", [mm(T[ps][0:H, h, i:384:16], T[src][:, 16 * H * h + i:16 * H * (h + 1):16], C(w), False, last and i == 15) for i in range(16)],
@@ -405,13 +487,14 @@ def rank_program(g, core, T, topo):
     def message(t, part):
         msg = "msg%d" % (t + 1)
         if part == 0:
-            same("eqt", T.ru[:, 0:K], "ru", ("lis", 0), "lis0")
-            ts(C("pari"), C("ni"), 1, Op.bitwise_and, "ni", "pari")
+            same("eqt", T.ru[:, 0:K], "rut0 rut1", ("lis", 0), "lisa0 lisa1")
+            ts(C("pari"), C("ni"), 1, Op.bitwise_and, "ni0 ni1", "pari")
             ts(C("w5"), C("pari"), -2.0, Op.mult, "pari", "w5", 1.0, Op.add)
-            tt(C("w6"), C("w5"), C("ni"), Op.add, "w5 ni", "w6")
+            tt(C("w6"), C("w5"), C("ni"), Op.add, "w5 ni0 ni1", "w6")
             tt(C("w5"), C("w6"), C("dm1"), Op.subtract, "w6 dm1", "w5")
             return
-        scan(T.sct2[:], T.psv[:, 0, 0:K], "psv0", "sct2")
+        lower("eqt", T.psd, "psd")
+        scan(T.sct2[:], T.psd[:, 0:K], "psd", "sct2")
         ts(C("z", 12, 24), T.sct2[:, 15:K:16], 0.0, Op.is_equal, "sct2", "z1")
         tt(C("dwin"), C("req"), C("z", 12, 24), Op.mult, "req z1", "dwin")
         tt(C("w6"), C("w5"), C("dwin"), Op.mult, "w5 dwin", "w6")
@@ -419,14 +502,14 @@ def rank_program(g, core, T, topo):
         mk = msg + " " + msg + "l"
         if t == 0:
             send(T[msg][:], mk, r - 1, T.up1[:], "ru1", "ls6")
+            arrives("ru1", NE, "up1", 7.0)
             send(T[msg][:], mk, r - 2, T.up2[:], "ru2", "ls7")
-            arrives("ru1", NE, "up1")
-            arrives("ru2", NE, "up2")
+            arrives("ru2", NE, "up2", 20.0)
         elif t == 1:
             send(T[msg][:], mk, r - 1, T.up3[:], "ru3", "ls8")
-            arrives("ru3", NE, "up3")
+            arrives("ru3", NE, "up3", 7.0)
         send(T[msg][:], mk, r + 1 + t, T["hm%d" % (t + 1)][:], "rh%d" % (t + 1), "ls%d" % (9 + t))
-        arrives("rh%d" % (t + 1), NE, "hm%d" % (t + 1))
+        arrives("rh%d" % (t + 1), NE, "hm%d" % (t + 1), (50.0, 20.0, 8.0)[t])
 
     L = lambda n: T[n][0:H, :, :]
     X = lambda n, i: T[n][0:H, :, 8 * i:8 * i + 8]
@@ -435,178 +518,164 @@ def rank_program(g, core, T, topo):
         lw, xl, msg = "lw%d" % j, "xl%d" % j, "msg%d" % j
         if t == 0:
             scalar_later()
-        for h in (0, 1):
-            pgather("pa", "lc", h)
         if t == 0:
             disks_out()
             weights()
-            for h in (0, 1):
-                xgather("ma", "lc", h)
-        for h in (0, 1):
-            op("p", [mm(T.psk[0:H, h, 0:384], T.ro2[0:1, 0:H], T.row[0:1, 0:384], True, False)], "ro2 row", "psk%d" % h)
-        for h in (0, 1):
-            if t:
-                xgather("ma", "lc", h)
-        if t:
-            ts(T.c16[:], T.cf[:], -2048.0, Op.add, "cf", "c16")
-        else:
             later()
-        for h in (0, 1):
-            sums("psk", *(("pa", "wp") if t else ("ma", "wm")), h)
-            sums("psk", *(("ma", "wm") if t else ("pa", "wp")), h)
-            op("p", [mm(T.psk[0:H, h, 128:256], T.c16[:, H * h:H * h + H], C("idh"), False, True)], "c16 idh", "psk%d" % h)
-        if t == 0:
             latest()
-            defer(claim_weights)
+            claim_weights()
             unpack(0)
+            unpack(1)
+            disk_window(1)
         elif t == 1:
             disk_window(2)
+            disk_window(3)
             apply("up1", "lw2")
-        else:
             apply("up2", "lw3")
-            apply("up3", "lw3")
-        act(L("co"), T.psk[0:H, :, 1:256:2], "psk0 psk1", "co")
-        tt(L("t1"), T.psk[0:H, :, 0:256:2], L("co"), Op.min, "psk0 psk1 co", "t1")
-        act(L("sl"), T.psk[0:H, :, 256:384], "psk0 psk1", "sl")
-        tt(L("t2"), T.t1[0:H, :, 0:128:2], T.t1[0:H, :, 1:128:2], Op.min, "t1", "t2")
-        tt(L("t3"), T.t2[0:H, :, 0:64:2], T.t2[0:H, :, 1:64:2], Op.min, "t2", "t3")
-        tt(L("t4"), T.t3[0:H, :, 0:32:2], T.t3[0:H, :, 1:32:2], Op.min, "t3", "t4")
-        ts(X("fi", 1), X("t4", 1), W - 1, Op.bitwise_and, "t4", "fi1")
-        ts(X("fi", 0), X("t4", 0), 2047, Op.bitwise_and, "t4", "fi0")
-        ts(X("fl", 1), X("fi", 1), -2048.0, Op.add, "fi1", "fl1")
-        cp(X("fl", 0), X("fi", 0), "fi0", "fl0")
-        halves(T.psg, T.fl, "fl0 fl1", "psg", 16, "idh")
-        cp(T.gt[0:16, :], T.psg[0:16, 0:K], "psg", "gt")
-        R16 = lambda f: C("rp", 128 * f, 128 * f + 128, p1=16)
-        op("p", [mm(T.psm[:, 0:K], R16(0), T.gt[0:16, :], True, False), mm(T.psm[:, 0:K], C("idb"), C("bm"), False, True)], "rp gt idb bm", "psm")
-        op("p", [mm(T.psu[:, K * f:K * f + K], R16(f), T.gt[0:16, :], True, True) for f in (0, 1)], "rp gt", "psu")
-        op("p", [mm(T.psk[:, 0, 0:K], R16(1), T.gt[0:16, :], True, False), mm(T.psk[:, 0, 0:K], C("idb"), C("bm"), False, True)], "rp gt idb bm", "psk0")
-        if t < 2:
-            disk_window(1 if t == 0 else 3)
         else:
+            apply("up3", "lw3")
             cp(T.lh[:, 0:M], T.lfi[:], "lfi", "lh")
-        scan(T.sct[:], T.psm[:, 0:K], "psm", "sct")
-        ts(C("ni"), T.sct[:, 15:K:16], 1, Op.logical_shift_right, "sct", "ni")
-        cp(C("ln"), C("ni"), "ni", "ln")
-        B = T[lw][:, 0:M]
-        act(T.sq[:, 0:K], B.indirect(C("ln")), lw + " ln", "sq0", AF.Square, bias=4.0)
-        act(T.sq[:, K:2 * K], B.indirect(C("ln")), lw + " ln", "sq1", AF.Square, bias=592.0)
-        op("v", [lambda: v.tensor_copy(T.b16[:], T[lw][:, 0:M].indirect(C("ln")))], lw + " ln", "b16")
-        act(T.at[:], T[xl][:].indirect(C("ln")), xl + " ln", "at")
-        ts(T.ru[:], T.psu[:, 0:2 * K], 2048.0, Op.add, "psu", "ru")
-        for c, (sc, of) in enumerate(((0.125, -2.4375), (0.03125, -10951.484375))):
-            ts(T.tt[:, K * c:K * c + K], T.sq[:, K * c:K * c + K], sc, Op.mult, "sq%d" % c, "tt%d" % c, of, Op.add)
-        for c in (0, 1):
-            ts(T.cc[:, K * c:K * c + K], T.tt[:, K * c:K * c + K], W - 1, Op.bitwise_and, "tt%d" % c, "cc%d" % c)
-        for c in (0, 1):
-            cp(T["l%d" % (c + 1)][:], T.cc[:, K * c:K * c + K], "cc%d" % c, "l%d" % (c + 1))
+        if t:
+            ts(T.c16[:], T.cf[:], -2048.0, Op.add, "cf", "c16")
+        R16 = lambda f: C("rp", 128 * f, 128 * f + 128, p1=16)
+        lnw = T[lw][:, 0:M]
         for h in (0, 1):
+            a, b, x, y = H * h, H * h + H, 6 * h, 6 * h + 6
+            k = lambda names: " ".join("%s%d" % (n, h) for n in names.split())
+            pgather("pa", "lc", "lc", h)
+            xgather("ma", "lc", "lc", h)
+            op("p", [mm(T.psk[0:H, h, 0:384], T.ro2[0:1, 0:H], T.row[0:1, 0:384], True, False)], "ro2 row", k("psk"))
+            sums("psk", *(("pa", "wp") if t else ("ma", "wm")), h)
+            sums("psk", *(("ma", "wm") if t else ("pa", "wp")), h)
+            op("p", [mm(T.psk[0:H, h, 128:256], T.c16[:, a:b], C("idh"), False, True)], "c16 idh", k("psk"))
+            act(T.co[0:H, h, :], T.psk[0:H, h, 1:256:2], k("psk"), k("co"))
+            tt(T.t1[0:H, h, :], T.psk[0:H, h, 0:256:2], T.co[0:H, h, :], Op.min, k("psk co"), k("t1_"))
+            act(T.sl[0:H, h, :], T.psk[0:H, h, 256:384], k("psk"), k("sl"))
+            tt(T.t2[0:H, h, :], T.t1[0:H, h, 0:128:2], T.t1[0:H, h, 1:128:2], Op.min, k("t1_"), k("t2_"))
+            tt(T.t3[0:H, h, :], T.t2[0:H, h, 0:64:2], T.t2[0:H, h, 1:64:2], Op.min, k("t2_"), k("t3_"))
+            tt(T.t4[0:H, h, :], T.t3[0:H, h, 0:32:2], T.t3[0:H, h, 1:32:2], Op.min, k("t3_"), k("t4_"))
+            ts(T.fi[0:H, h, 8:16], T.t4[0:H, h, 8:16], W - 1, Op.bitwise_and, k("t4_"), k("fio"))
+            ts(T.fi[0:H, h, 0:8], T.t4[0:H, h, 0:8], 2047, Op.bitwise_and, k("t4_"), k("fit"))
+            ts(T.fl[0:H, h, 8:16], T.fi[0:H, h, 8:16], -2048.0, Op.add, k("fio"), k("flo"))
+            cp(T.fl[0:H, h, 0:8], T.fi[0:H, h, 0:8], k("fit"), k("flt"))
+            op("p", [mm(T.psk[0:16, h, 384:480], T.fl[0:H, h, :], C("idh", 0, H, p1=H), True, True)], k("flo flt") + " idh", k("psk"))
+            cp(T.gt[0:16, a:b], T.psk[0:16, h, 384:480], k("psk"), k("gt"))
+            pb, pk = ((T.psm, "psm"), (T.psu, "psu"))[h]
+            fs = []
+            for f in (0, 1):
+                fs += [mm(pb[:, H * f:H * f + H], R16(f), T.gt[0:16, a:b], True, False), mm(pb[:, H * f:H * f + H], C("idb"), C("bm", 0, H), False, True),
+                       mm(pb[:, H * f + K:H * f + K + H], R16(f), T.gt[0:16, a:b], True, True)]
+            op("p", fs, "rp idb bm " + k("gt"), pk)
+            scan(T.sct[:, a:b], pb[:, 0:H], pk, k("sct"), H)
+            ts(C("ni", x, y), T.sct[:, a + 15:b:16], 1, Op.logical_shift_right, k("sct"), k("ni"))
+            cp(C("ln", x, y), C("ni", x, y), k("ni"), k("ln"))
+            LN = C("ln", x, y)
+            act(T.sq[:, a:b], lnw.indirect(LN), lw + " " + k("ln"), k("sqa"), AF.Square, bias=4.0)
+            act(T.sq[:, K + a:K + b], lnw.indirect(LN), lw + " " + k("ln"), k("sqb"), AF.Square, bias=592.0)
+            cp(T.b16[:, a:b], lnw.indirect(LN), lw + " " + k("ln"), k("b16_"))
+            if h == 0:
+                features(j)
+            act(T.at[:, a:b], T[xl][:].indirect(LN), xl + " xh%d " % j + k("ln"), k("at"))
+            for c, (sc, of) in enumerate(((0.125, -2.4375), (0.03125, -10951.484375))):
+                u, w, n = K * c + a, K * c + b, "ab"[c]
+                ts(T.tt[:, u:w], T.sq[:, u:w], sc, Op.mult, k("sq" + n), k("tt" + n), of, Op.add)
+                ts(T.cc[:, u:w], T.tt[:, u:w], W - 1, Op.bitwise_and, k("tt" + n), k("cc" + n))
+                cp(T["l%d" % (c + 1)][:, a:b], T.cc[:, u:w], k("cc" + n), k("li" + n))
+            scan(T.sco[:, a:b], pb[:, H:K], pk, k("sco"), H)
+            ts(T.ru[:, a:b], pb[:, K:K + H], 2048.0, Op.add, pk, k("rut"))
+            ts(T.ru[:, K + a:K + b], pb[:, K + H:2 * K], 2048.0, Op.add, pk, k("ruo"))
+            ts(C("lis", 12 + x, 12 + y), T.sco[:, a + 15:b:16], 2048.0, Op.add, k("sco"), k("lisb"))
+            ts(C("lis", x, y), T.sct[:, a + 15:b:16], 2048.0, Op.add, k("sct"), k("lisa"))
             op("p", [mm(T.psv[0:H, h, :], T.ro2[32:33, 0:H], T.row[32:33, :], True, False),
-                     mm(T.psv[0:H, h, 128:512], T.b16[:, H * h:H * h + H], C("bi"), False, False)], "ro2 row1 b16 bi", "psv%d" % h)
+                     mm(T.psv[0:H, h, 128:512], T.b16[:, a:b], C("bi"), False, False)], "ro2 row1 bi " + k("b16_"), k("psv"))
         for h in (0, 1):
-            pgather("pa", "l1", h)
-            pgather("pb", "l2", h)
-        xgather("ma", "l1", 0)
-        sums("psv", "ma", "wm1", 0)
-        sums("psv", "pa", "wp1", 0)
-        scan(T.sco[:], T.psk[:, 0, 0:K], "psk0", "sco")
-        ts(C("lis", 12, 24), T.sco[:, 15:K:16], 2048.0, Op.add, "sco", "lis1")
-        ts(C("lis", 0, 12), T.sct[:, 15:K:16], 2048.0, Op.add, "sct", "lis0")
-        cp(C("lo"), C("lis", 12, 24), "lis1", "lo")
-        same("eqo", T.ru[:, K:2 * K], "ru", ("lis", 12), "lis1")
+            for c in "ab":
+                pgather("p" + c, "l%d" % ("ab".index(c) + 1), "li%s%d" % (c, h), h)
+                xgather("m" + c, "l%d" % ("ab".index(c) + 1), "li%s%d" % (c, h), h)
+                sums("psv", "m" + c, "wm%d" % ("ab".index(c) + 1), h)
+                sums("psv", "p" + c, "wp%d" % ("ab".index(c) + 1), h, c == "b")
+        cp(C("lo"), C("lis", 12, 24), "lisb0 lisb1", "lo")
+        same("eqo", T.ru[:, K:2 * K], "ruo0 ruo1", ("lis", 12), "lisb0 lisb1")
         lower("eqo", T.psd, "psd")
-        xgather("mb", "l2", 0)
-        defer(lambda: message(t, 0))
+        message(t, 0)
         scan(T.scd[:], T.psd[:, 0:K], "psd", "scd")
-        ts(C("ei"), T.sct[:, 15:K:16], 1, Op.bitwise_and, "sct", "ei")
+        ts(C("ei"), T.sct[:, 15:K:16], 1, Op.bitwise_and, "sct0 sct1", "ei")
         ts(C("z", 0, 12), T.scd[:, 15:K:16], 0.0, Op.is_equal, "scd", "z0")
-        tt(C("w1"), C("lis", 12, 24), C("dm4"), Op.subtract, "lis1 dm4", "w1")
+        tt(C("w1"), C("lis", 12, 24), C("dm4"), Op.subtract, "lisb0 lisb1 dm4", "w1")
         tt(C("cand"), C("z", 0, 12), C("ei"), Op.mult, "z0 ei", "cand")
         op("v", [lambda: v.tensor_tensor_scan(C("exb", 1, 13), C("one", 0, 12), C("cand"), 0.0, Op.mult, Op.add)], "one cand", "exb")
-        xgather("ma", "l1", 1)
-        op("p", [mm(T.psk[:, 1, 400:412], C("bt"), C("cand"), True, False), mm(T.psk[:, 1, 400:412], C("blb"), C("exb", 0, 12), False, True)], "bt cand blb exb", "psk1")
-        halves(T.psk[:, 1, :], T.sl, "sl", "psk1", 128, "idf")
-        sums("psv", "mb", "wm2", 0)
-        sums("psv", "pb", "wp2", 0, True)
-        ts(C("rk"), T.psk[:, 1, 400:412], float(CAP), Op.is_le, "psk1", "rk")
-        tt(T.dc[:], T.cc[:, K:2 * K], T.cc[:, 0:K], Op.subtract, "cc0 cc1", "dc")
+        op("p", [mm(T.psg[:, 400:412], C("bt"), C("cand"), True, False), mm(T.psg[:, 400:412], C("blb"), C("exb", 0, 12), False, True)], "bt cand blb exb", "psg")
+        ts(C("rk"), T.psg[:, 400:412], float(CAP), Op.is_le, "psg", "rk")
+        halves(T.psk[:, 1, :], T.sl, "sl0 sl1", "psk1", 128, "idf")
+        tt(T.dc[:], T.cc[:, K:2 * K], T.cc[:, 0:K], Op.subtract, "cca0 cca1 ccb0 ccb1", "dc")
         tt(C("req"), C("rk"), C("cand"), Op.mult, "rk cand", "req")
         tt(C("w2"), C("w1"), C("req"), Op.mult, "w1 req", "w2")
         ts(C("nrq"), C("req"), -8192.0, Op.mult, "req", "nrq", 8192.0 + 2048.0, Op.add)
         tt(C("ld"), C("w2"), C("dm4"), Op.add, "w2 dm4", "ld")
-        xgather("mb", "l2", 1)
-        for c, w in (("a", "1"), ("b", "2")):
-            sums("psv", "m" + c, "wm" + w, 1)
-            sums("psv", "p" + c, "wp" + w, 1, c == "b")
-        if t == 0:
-            flush()
         act(T[msg][:, 0:K], T.psk[:, 1, 0:K], "psk1", msg)
+        message(t, 1)
         act(T.g2[:], T.pw[:].indirect(C("ld")), PW + " ld", "g2")
         op("p", [mm(T.psk[:, 0, 0:K], C("sa"), T.at[:], True, False), mm(T.psk[:, 0, 0:K], C("dg1"), T.g2[:], False, False),
-                 mm(T.psk[:, 0, 0:K], T.row[96:97, 128 * t:128 * t + 128], T.ro2[96:97, 0:K], False, True)], "sa at dg1 g2 row3 ro2", "psk0")
+                 mm(T.psk[:, 0, 0:K], T.row[96:97, 128 * t:128 * t + 128], T.ro2[96:97, 0:K], False, True)], "sa at0 at1 dg1 g2 row3 ro2", "psk0")
         act(T.v2[:], T.psk[:, 0, 0:K], "psk0", "v2")
-        op("v", [lambda: v.tensor_copy(T.xw[:].indirect(C("ld")), T.at[:])], "ld at", XW)
-        PV = "psv0 psv1"
-        ts(L("r1"), T.psv[0:H, :, 128:256], 0.0, Op.is_equal, PV, "r1", -4096.0, Op.mult)
-        ts(T.psv[0:H, :, 256:384], T.psv[0:H, :, 256:384], 0.0, Op.is_equal, PV, PV + " r2", 1024.0, Op.mult)
-        tt(L("u1"), T.psv[0:H, :, 0:128], L("r1"), Op.add, PV + " r1", "u1")
-        tt(L("u2"), T.psv[0:H, :, 256:384], L("u1"), Op.add, PV + " u1 r2", "u2")
-        act(L("ub"), L("u2"), "u2", "ub", AF.Abs)
-        ts(L("pk"), L("u2"), 0.0, Op.is_gt, "u2", "pk")
-        halves(T.psg, T.pk, "pk", "psg", 128, "idb")
-        tt(L("kk"), T.psv[0:H, :, 384:512], L("pk"), Op.add, PV + " pk", "kk")
-        ts(T.psv[0:H, :, 128:256], L("ub"), 512.0, Op.is_gt, "ub r1", PV + " r3", RES, Op.mult)
-        tt(L("k2"), T.psv[0:H, :, 128:256], L("kk"), Op.add, PV + " kk r3", "k2")
-        tt(L("ka"), T.k2[0:H, :, 0:128:2], T.k2[0:H, :, 1:128:2], Op.min, "k2", "ka")
-        tt(L("kb"), T.ka[0:H, :, 0:64:2], T.ka[0:H, :, 1:64:2], Op.min, "ka", "kb")
-        tt(L("kc"), T.kb[0:H, :, 0:32:2], T.kb[0:H, :, 1:32:2], Op.min, "kb", "kc")
-        tt(L("kd"), T.kc[0:H, :, 0:16:2], T.kc[0:H, :, 1:16:2], Op.min, "kc", "kd")
-        ts(X("t4", 0), L("kd"), 1, Op.logical_shift_right, "kd", "t4", 1023, Op.bitwise_and)
-        ts(X("t4", 1), L("kd"), 6, Op.logical_shift_right, "kd", "t4p", 31, Op.bitwise_and)
-        ts(X("fg", 0), X("t4", 0), 4.0, Op.add, "t4", "fg0")
-        ts(X("fg", 1), X("t4", 0), 592.0, Op.add, "t4", "fg1")
-        ts(X("fh", 0), L("kd"), 1, Op.bitwise_and, "kd", "fh")
-        tt(T.t3[0:H, :, 0:16], L("fg"), L("fg"), Op.mult, "fg0 fg1", "t3")
-        cp(T.fm[0:H, :, 16:32], L("t4"), "t4 t4p", "fm1")
-        ts(X("fi", 0), X("t3", 0), 0.125, Op.mult, "t3", "fi0", -2.4375, Op.add)
-        ts(X("fi", 1), X("t3", 1), 0.03125, Op.mult, "t3", "fi1", -10951.484375, Op.add)
-        ts(X("fm", 1), L("kd"), RES, Op.is_ge, "kd", "fm2")
-        ts(L("fe"), L("fi"), W - 1, Op.bitwise_and, "fi0 fi1", "fe")
-        tt(X("t2", 1), X("fe", 1), X("fe", 0), Op.subtract, "fe", "t2")
-        ts(X("t2", 0), X("fe", 0), -2048.0, Op.add, "fe", "t2b")
-        tt(X("t2", 2), X("t2", 1), X("fh", 0), Op.mult, "t2 fh", "t2c")
-        tt(X("fm", 0), X("t2", 2), X("t2", 0), Op.add, "t2c t2b", "fm0")
-        flush()
+        cp(T.xw[:].indirect(C("ld")), T.at[:], "ld at0 at1", XW)
+        for h in (0, 1):
+            k = lambda names: " ".join("%s%d" % (n, h) for n in names.split())
+            U = lambda n: T[n][0:H, h, :]
+            ts(U("r1"), T.psv[0:H, h, 128:256], 0.0, Op.is_equal, k("psv"), k("ra"), -4096.0, Op.mult)
+            ts(T.psv[0:H, h, 256:384], T.psv[0:H, h, 256:384], 0.0, Op.is_equal, k("psv"), k("rb psv"), 1024.0, Op.mult)
+            tt(U("u1"), T.psv[0:H, h, 0:128], U("r1"), Op.add, k("psv ra"), k("ua"))
+            tt(U("u2"), T.psv[0:H, h, 256:384], U("u1"), Op.add, k("psv ua rb"), k("uc"))
+            act(U("ub"), U("u2"), k("uc"), k("ub"), AF.Abs)
+            ts(U("pk"), U("u2"), 0.0, Op.is_gt, k("uc"), k("pk"))
+            tt(U("kk"), T.psv[0:H, h, 384:512], U("pk"), Op.add, k("psv pk"), k("kk"))
+            ts(T.psv[0:H, h, 128:256], U("ub"), 512.0, Op.is_gt, k("ub ra"), k("rc psv"), RES, Op.mult)
+            tt(U("k2"), T.psv[0:H, h, 128:256], U("kk"), Op.add, k("psv kk rc"), k("kz"))
+            tt(U("ka"), T.k2[0:H, h, 0:128:2], T.k2[0:H, h, 1:128:2], Op.min, k("kz"), k("ka"))
+            tt(U("kb"), T.ka[0:H, h, 0:64:2], T.ka[0:H, h, 1:64:2], Op.min, k("ka"), k("kb"))
+            tt(U("kc"), T.kb[0:H, h, 0:32:2], T.kb[0:H, h, 1:32:2], Op.min, k("kb"), k("kc"))
+            tt(U("kd"), T.kc[0:H, h, 0:16:2], T.kc[0:H, h, 1:16:2], Op.min, k("kc"), k("kd"))
+        halves(T.psg, T.pk, "pk0 pk1", "psg", 128, "idb")
+        KD = "kd0 kd1"
+        ts(X("t7", 0), L("kd"), 1, Op.logical_shift_right, KD, "t7", 1023, Op.bitwise_and)
+        ts(X("t7", 1), L("kd"), 6, Op.logical_shift_right, KD, "t7p", 31, Op.bitwise_and)
+        ts(X("fg", 0), X("t7", 0), 4.0, Op.add, "t7", "fga")
+        ts(X("fg", 1), X("t7", 0), 592.0, Op.add, "t7", "fgb")
+        ts(X("fh", 0), L("kd"), 1, Op.bitwise_and, KD, "fh")
+        tt(L("t5"), L("fg"), L("fg"), Op.mult, "fga fgb", "t5")
+        cp(T.fm[0:H, :, 16:32], L("t7"), "t7 t7p", "fm1")
+        ts(X("fj", 0), X("t5", 0), 0.125, Op.mult, "t5", "fja", -2.4375, Op.add)
+        ts(X("fj", 1), X("t5", 1), 0.03125, Op.mult, "t5", "fjb", -10951.484375, Op.add)
+        ts(X("fm", 1), L("kd"), RES, Op.is_ge, KD, "fm2")
+        ts(L("fe"), L("fj"), W - 1, Op.bitwise_and, "fja fjb", "fe")
+        tt(X("t6", 1), X("fe", 1), X("fe", 0), Op.subtract, "fe", "t6")
+        ts(X("t6", 0), X("fe", 0), -2048.0, Op.add, "fe", "t6b")
+        tt(X("t6", 2), X("t6", 1), X("fh", 0), Op.mult, "t6 fh", "t6c")
+        tt(X("fm", 0), X("t6", 2), X("t6", 0), Op.add, "t6c t6b", "fm0")
         halves(T.psm, T.fm, "fm0 fm1 fm2", "psm", 32, "idh")
-        lower("eqt", T.psv[:, 0, :], "psv0")
         tt(T.sp[:], T.psg[:, 0:K], T.dc[:], Op.mult, "psg dc", "sp")
         cp(T.gu[0:32, :], T.psm[0:32, 0:K], "psm", "gu")
         op("p", [mm(T.psu[:, 0:K], C("rpc", p1=32), T.gu[0:32, :], True, True)], "rpc gu", "psu")
         op("p", [mm(T.psg[:, 0:K], C("rpc", p1=32), T.gu[0:32, :], True, False), mm(T.psg[:, 0:K], C("idb"), C("bm"), False, True)], "rpc gu idb bm", "psg")
-        tt(T.sg[:], T.sp[:], T.cc[:, 0:K], Op.add, "sp cc0", "sg")
-        op("v", [lambda: v.tensor_copy(T.pw[:].indirect(C("ld")), T.v2[:])], "ld v2", PW)
-        ts(T.ru2[:], T.psu[:, 0:K], 2048.0, Op.add, "psu", "ru2")
-        scan(T.sco[:], T.psg[:, 0:K], "psg", "sco")
-        tt(C("pls"), C("nrq"), T.sco[:, 15:K:16], Op.add, "nrq sco", "pls")
-        same("eqo", T.ru2, "ru2", ("pls", 0), "pls")
+        tt(T.sg[:], T.sp[:], T.cc[:, 0:K], Op.add, "sp cca0 cca1", "sg")
+        cp(T.pw[:].indirect(C("ld")), T.v2[:], "ld v2", PW)
+        ts(T.ru2[:], T.psu[:, 0:K], 2048.0, Op.add, "psu", "ru2_")
+        scan(T.scl[:], T.psg[:, 0:K], "psg", "scl")
+        tt(C("pls"), C("nrq"), T.scl[:, 15:K:16], Op.add, "nrq scl", "pls")
+        same("eqo", T.ru2, "ru2_", ("pls", 0), "pls")
         lower("eqo", T.psd, "psd")
         ts(C("w3"), C("pls"), float(W), Op.is_lt, "pls", "w3")
         tt(C("w4"), C("pls"), C("dm4"), Op.subtract, "pls dm4", "w4")
-        if t == 0:
-            unpack(1)
-        op("v", [lambda: v.tensor_copy(T.fw[:].indirect(C("ld")), T.sg[:])], "ld sg", FW)
+        cp(T.fw[:].indirect(C("ld")), T.sg[:], "ld sg", FW)
         tt(C("w2"), C("w3"), C("w4"), Op.mult, "w3 w4", "w2")
-        op("v", [lambda: v.tensor_tensor(T.qs[:], T.xw[:, 0:W].indirect(C("lo")), T.q[:], Op.add)], XW + " lo q", "qs")
-        op("v", [lambda: v.tensor_copy(T.cf[:], T.fw[:, 0:W].indirect(C("lo")))], FW + " lo", "cf")
+        tt(T.qs[:], T.xw[:, 0:W].indirect(C("lo")), T.q[:], Op.add, XW + " lo q", "qs")
+        cp(T.cf[:], T.fw[:, 0:W].indirect(C("lo")), FW + " lo", "cf")
         ts(T.qb[:], T.qs[:], 0.5, Op.mult, "qs", "qb", 127.8125, Op.add)
         if t < RO - 1:
             cp(T.lc[:], T.cf[:], "cf", "lc")
             for i in range(16):
-                if i % 8 in (1, 4, 6):
-                    act(T.qrep[:, i:16 * K:16], T.qb[:], "qb", "qr%d" % i, AF.Copy, bias=-128.0)
-                else:
-                    defer(lambda: ts(T.qrep[:, i:16 * K:16], T.qb[:], -128.0, Op.add, "qb", "qr%d" % i))
-        defer(lambda: ts(T.q[:], T.qb[:], -128.0, Op.add, "qb", "q"))
+                ts(T.qrep[:, i:16 * K:16], T.qb[:], -128.0, Op.add, "qb", "qr%d" % i)
+        ts(T.q[:], T.qb[:], -128.0, Op.add, "qb", "q")
         scan(T.scd[:], T.psd[:, 0:K], "psd", "scd")
         ts(C("z", 0, 12), T.scd[:, 15:K:16], 0.0, Op.is_equal, "scd", "z0")
         tt(C("w1"), C("w2"), C("z", 0, 12), Op.mult, "w2 z0", "w1")
@@ -616,9 +685,7 @@ def rank_program(g, core, T, topo):
                  mm(T.psm[:, 0:K], T.row[0:1, 384:512], T.ro2[0:1, 0:K], False, False),
                  mm(T.psm[:, 0:K], C("dgc%d" % t), T.g1[:], False, True)], "vr gu row2 ro2 dgc%d g1" % t, "psm")
         act(T.v1[:], T.psm[:, 0:K], "psm", "v1")
-        flush()
-        op("v", [lambda: v.tensor_copy(T.pw[:].indirect(C("lcl")), T.v1[:])], "lcl v1", PW)
-        message(t, 1)
+        cp(T.pw[:].indirect(C("lcl")), T.v1[:], "lcl v1", PW)
         if t == 1:
             yt_weights()
     dma("d", T.yc[:], T.cf[:], "cf", "yc")

from concourse.mybir import AluOpType as Op, ActivationFunctionType as AF

W, M, K, CAP, RO, N = 4096, 1024, 192, 160, 3, 8
H = 96
BIG = 65536.0
RES = 1048576.0
NE = 8
WAKE, SLACK = 0.3, 0.1
VCOST = {"ma": 1.7, "mb": 1.7, "xw": 0.6, "pw": 0.6, "fw": 0.7, "lw": 0.7, "lh": 0.7, "lfu": 0.85, "pcs": 0.64, "sq": 0.2, "cf": 0.25, "qs": 0.25, "eqo": 0.07, "eqt": 0.07, "cc": 0.12, "dc": 0.32, "sp": 0.16, "sg": 0.32, "u": 0.11}
SCOST = {"pa": 1.7, "pb": 1.7, "pw": 0.43, "g": 0.28, "at": 0.15, "wt": 0.06, "ltk": 0.11, "wm": 0.06, "wp": 0.06}

_S = "sbuf"
F32, B16, I32, U16, H16 = "float32", "bfloat16", "int32", "uint16", "float16"
PACK = {
    "tf": (F32, (("z", 24), ("lis", 24), ("req", 12), ("rk", 12), ("dwin", 12), ("w1", 12), ("w2", 12), ("w3", 12), ("w4", 12), ("w5", 12), ("w6", 12), ("nrq", 12), ("pls", 12),
                 ("dm4", 12), ("dm1", 12), ("er", 24), ("lt", 16), ("pmf", 4))),
    "tl": (U16, (("ln", 12), ("lo", 12), ("ld", 12), ("lcl", 12), ("lm", 12))),
    "ti": (I32, (("ni", 12), ("ei", 12), ("pari", 12), ("dmi", 12), ("pmi", 4))),
    "tb": (B16, (("wm", 24), ("wp", 24), ("wm1", 24), ("wm2", 24), ("wp1", 24), ("wp2", 24), ("cand", 12), ("exb", 16))),
    "cb": (B16, (("idb", 128), ("blb", 128), ("bt", 128), ("dg1", 128), ("sa", 128), ("dgc0", 128), ("dgc1", 128), ("dgc2", 128), ("bm", K), ("ltk", 2048), ("pb16", 128), ("nb16", 128))),
    "cff": (F32, (("one", 512), ("idf", 128), ("blf", 128), ("btf", 128), ("af0", 128), ("af1", 128), ("af2", 128), ("sam", 384), ("rpf", 512), ("vrf", 384))),
    "chh": (H16, (("rp", 512), ("rpc", 128), ("vr", 128), ("bi", 384), ("idh", 128))),
}
PLACE, SCRATCH = {}, {}
for _b in PACK:
    _o = 0
    for _n, _w in PACK[_b][1]:
        PLACE[_n] = (_b, _o, _w)
        _o += _w
    SCRATCH[_b] = (_S, [128, _o], PACK[_b][0])
for _d, _l in (
    (B16, (("xw", W + K), ("pw", W + K), ("pcs", 768), ("xlh", M), ("q", K), ("qb", K), ("qrep", 16 * K), ("ma", 16 * K), ("mb", 16 * K), ("pa", 16 * K), ("pb", 16 * K),
           ("at", K), ("g1", K), ("v1", K), ("g2", K), ("v2", K), ("row", 512), ("ro2", 512), ("wt", 512), ("xl1", M), ("xl2", M), ("xl3", M), ("xp1", 512), ("xp2", 512), ("xp3", 512), ("xlp", 512), ("xt", 512))),
    (I32, (("fw", W + K), ("fdt", 2048), ("tgs", 256), ("pci", 768), ("lfi", M), ("cxi", K), ("sct", K), ("sco", K), ("scl", K), ("tt", 2 * K), ("cc", 2 * K), ("dc", K), ("sg", K), ("ia", K), ("ic", 512))),
    (U16, (("lfu", M), ("lc", K), ("ru", 2 * K), ("ru2", K), ("l1", K), ("l2", K), ("lu1", M), ("lu2", M), ("lu3", M))),
    (F32, (("lh", M + K), ("qs", K), ("cf", K), ("scd", K), ("sct2", K), ("sq", 2 * K), ("sp", K), ("yts", 512), ("s0", K), ("lw1", M), ("lw2", M + K), ("lw3", M + K),
           ("msg1", K + 12), ("msg2", K + 12), ("msg3", K + 12), ("up1", K + 12), ("up2", K + 12), ("up3", K + 12), ("hm1", K + 12), ("hm2", K + 12), ("hm3", K + 12))),
    (H16, (("gt", K), ("gu", K), ("b16", K), ("c16", K))),
):
    for _n, _w in _l:
        SCRATCH[_n] = (_S, [128, _w], _d)
for _n, _w, _d in (("co", 128, F32), ("t1", 128, F32), ("t2", 64, F32), ("t3", 32, F32), ("t4", 16, I32), ("fi", 16, I32), ("fl", 16, H16), ("sl", 128, F32), ("r1", 128, F32), ("r2", 128, F32), ("u1", 128, F32),
                   ("u2", 128, F32), ("ub", 128, F32), ("pk", 128, B16), ("kk", 128, F32), ("k2", 128, F32), ("ka", 64, F32), ("kb", 32, F32), ("kc", 16, F32), ("kd", 8, I32), ("fe", 16, I32), ("fg", 16, F32), ("fh", 16, I32), ("fm", 32, H16), ("t5", 16, F32), ("t6", 32, F32), ("t7", 16, I32), ("fj", 16, I32)):
    SCRATCH[_n] = (_S, [128, 2, _w], _d)
SCRATCH["eqo"] = (_S, [128, 12, K], B16)
SCRATCH["eqt"] = (_S, [128, 12, K], B16)
for _n in ("psk", "psv"):
    SCRATCH[_n] = ("psum", [128, 2, 512], F32)
for _n in ("psm", "psu", "psd", "psg"):
    SCRATCH[_n] = ("psum", [128, 512], F32)
SEMAPHORES = ["qv", "qs", "qp", "qg"] + ["ld%d" % j for j in range(20)] + ["ls%d" % j for j in range(16)]
SEMAPHORES += ["%s%d" % (a, j) for a in ("rl", "rx", "ru", "rh") for j in (1, 2, 3)]


def tracker(g, T):
    Q = {"v": g.vector, "s": g.scalar, "p": g.tensor, "g": g, "d": g.sync}
    cnt = {"v": 0, "s": 0, "p": 0, "g": 0}
    known = {q: {} for q in Q}
    hist, wr, rd, total = {}, {}, {}, {}
    nd = [0]

    def learn(q, sem, val):
        if known[q].get(sem, 0) < val:
            known[q][sem] = val
        for s2, v2 in hist.get((sem, val), {}).items():
            if known[q].get(s2, 0) < v2:
                known[q][s2] = v2

    def needs(q, comp, R, Wt):
        out = []
        for k in R:
            if k in wr:
                out.append((k, wr[k]))
            if k.startswith("ps"):
                out += [(k, x) for x in rd.get(k, {}).values()]
        for k in Wt:
            if k in wr:
                out.append((k, wr[k]))
            out += [(k, x) for x in rd.get(k, {}).values()]
        need = {}
        for k, (sem, val, dq) in out:
            if comp and dq == q and (q == "p" or k.startswith("ps")):
                continue
            if need.get(sem, 0) < val:
                need[sem] = val
        return need

    def deps(q, comp, R, Wt):
        need = needs(q, comp, R, Wt)
        for sem in sorted(need, key=lambda s: -len(hist.get((s, need[s]), {}))):
            if known[q].get(sem, 0) < need[sem]:
                Q[q].wait_ge(T.sem[sem], need[sem])
                learn(q, sem, need[sem])

    def note(ev, q, R, Wt):
        for k in Wt:
            wr[k] = ev
            rd[k] = {}
        for k in R:
            rd.setdefault(k, {})[ev[0] if ev[2] is None else q] = ev

    def op_(q, fns, R, Wt):
        R, Wt = R.split(), Wt.split()
        deps(q, True, R, Wt)
        for f in fns[:-1]:
            f()
        sem = "q" + q
        cnt[q] += 1
        fns[-1]().then_inc(T.sem[sem], 1)
        total[sem] = cnt[q]
        hist[(sem, cnt[q])] = dict(known[q])
        if cnt[q] > 1:
            hist[(sem, cnt[q])][sem] = cnt[q] - 1
        note((sem, cnt[q], q), q, R, Wt)

    def dma_(q, out, in_, R, Wt):
        R, Wt = R.split(), Wt.split()
        deps(q, False, R, Wt)
        sem = "ld%d" % nd[0]
        nd[0] += 1
        Q[q].dma_start(out, in_).then_inc(T.sem[sem], 16)
        total[sem] = 16
        hist[(sem, 16)] = dict(known[q])
        note((sem, 16, None), q, R, Wt)

    def send_(call, R, local, n):
        deps("g", False, R.split(), [])
        call()
        total[local] = n
        note((local, n, None), "g", R.split(), [])

    def arrives_(sem, n, key):
        total[sem] = n
        wr[key] = (sem, n, None)
        rd[key] = {}

    nodes = []

    def op(q, fns, R="", Wt=""):
        nodes.append((q, R.split(), Wt.split(), lambda: op_(q, fns, R, Wt), len(fns), 0.0, -1))

    def dma(q, out, in_, R="", Wt="", lat=2.2):
        nodes.append((q, R.split(), Wt.split(), lambda: dma_(q, out, in_, R, Wt), 0, lat, -1))

    def send(call, R, local, n):
        nodes.append(("g", R.split(), [], lambda: send_(call, R, local, n), 0, 0.0, -1))

    def arrives(sem, n, key, lat):
        nodes.append(("a", [], [key], lambda: arrives_(sem, n, key), 0, lat, len(nodes) - 1))

    def cost(q, W1, n):
        if q == "p":
            return 0.05 * n
        if n == 0:
            return 0.3 if q == "g" else 0.1
        if q == "g":
            return 0.6
        return (SCOST if q == "s" else VCOST).get(W1, 0.2 if q == "s" else 0.09)

    def finish():
        nn = len(nodes)
        dep = [set() for _ in nodes]
        w, rds, ps = {}, {}, {}
        for x, (q, R, Wt, f, n, lat, after) in enumerate(nodes):
            if after >= 0:
                dep[x].add(after)
            for k in sorted(set(R + Wt)):
                if k.startswith("ps"):
                    cur = ps.setdefault(k, [q, [], []])
                    if cur[0] == q:
                        dep[x].update(cur[2])
                        if q == "p" and cur[1]:
                            dep[x].add(cur[1][-1])
                        cur[1].append(x)
                    else:
                        dep[x].update(cur[1])
                        ps[k] = [q, [x], cur[1]]
                    continue
                if k in w:
                    dep[x].add(w[k])
                if k in Wt:
                    dep[x].update(rds.get(k, []))
            for k in Wt:
                w[k], rds[k] = x, []
            for k in R:
                if k not in Wt:
                    rds.setdefault(k, []).append(x)
            dep[x].discard(x)
        succ = [[] for _ in nodes]
        for x in range(nn):
            for d in dep[x]:
                succ[d].append(x)
        cs = [0.0 if nd_[0] == "a" else cost(nd_[0], (nd_[2] + nd_[1] + [""])[0].rstrip("0123456789"), nd_[4]) for nd_ in nodes]
        pr = [0.0] * nn
        for x in range(nn - 1, -1, -1):
            pr[x] = cs[x] + nodes[x][5] + max([pr[y] + WAKE for y in succ[x]] + [0.0])
        left = [len(d) for d in dep]
        ready = {q: [] for q in "vspgda"}
        fin, qt = [0.0] * nn, {q: 0.0 for q in "vspgda"}
        early = [0.0] * nn
        for x in range(nn):
            if not left[x]:
                ready[nodes[x][0]].append(x)
        for _ in range(nn):
            best = None
            for q in "avspgd":
                if not ready[q]:
                    continue
                st = {}
                for x in ready[q]:
                    e = early[x]
                    st[x] = e if q == "a" else (e + WAKE if e > qt[q] - 0.001 else qt[q])
                lo = min(st.values())
                if q in "gd":
                    x = min(ready[q])
                else:
                    x = max((y for y in st if st[y] <= lo + SLACK), key=lambda y: (pr[y], -y))
                if best is None or st[x] < best[0]:
                    best = (st[x], q, x)
            t0, q, x = best
            ready[q].remove(x)
            e = t0 + cs[x]
            qt[q] = e
            fin[x] = e + nodes[x][5]
            nodes[x][3]()
            for y in succ[x]:
                left[y] -= 1
                early[y] = max(early[y], fin[x])
                if not left[y]:
                    ready[nodes[y][0]].append(y)
        for sem in total:
            if known["g"].get(sem, 0) < total[sem]:
                g.wait_ge(T.sem[sem], total[sem])
                learn("g", sem, total[sem])
    return op, dma, send, arrives, finish


def rank_program(g, core, T, topo):
    r = T.rank_of(core)
    if r is None:
        return
    v, s, p = g.vector, g.scalar, g.tensor
    op, dma, put, arrives, finish = tracker(g, T)

    def C(n, a=0, b=None, p0=0, p1=128, st=1):
        bf, o, w = PLACE[n]
        return T[bf][p0:p1, o + a:o + (w if b is None else b):st]

    def tt(o, a, b, f, R, Wt):
        op("v", [lambda: v.tensor_tensor(o, a, b, f)], R, Wt)

    def ts(o, a, x, f, R, Wt, y=None, f2=None):
        if f2 is None:
            op("v", [lambda: v.tensor_scalar(o, a, x, None, f)], R, Wt)
        else:
            op("v", [lambda: v.tensor_scalar(o, a, x, y, f, f2)], R, Wt)

    def cp(o, a, R, Wt):
        op("v", [lambda: v.tensor_copy(o, a)], R, Wt)

    def fill(o, c, Wt):
        op("v", [lambda: v.memset(o, c)], "", Wt)

    def act(o, a, R, Wt, f=AF.Identity, **kw):
        op("s", [lambda: s.activation(o, a, f, **kw)], R, Wt)

    def mm(o, l, x, st, sp):
        return lambda: p.matmul(o, l, x, st, sp)

    def scan(o, d, R, Wt, n=K):
        op("v", [lambda: v.tensor_tensor_scan(o, T.s0[:, 0:n], d, 0.0, Op.add, Op.min)], R + " s0", Wt)

    def send(src, key, dst_rank, dst, sem, local, bulk=False):
        dst_core = T.cores[dst_rank % N]
        rid, pid = topo.addr(dst_core)[0:2]
        eng = topo.engines(core, dst_core)
        eng = eng[-NE:] if bulk else eng[0:NE]
        put(lambda: g.remote_dma(dst, src, T.sem[sem], T.sem[local], pid, rid, sum(1 << e for e in eng)), key, local, len(eng))

    PWI = " ".join("pw%d" % c for c in range(8))
    PW = PWI + " pwr0 pwr1 pwr2 pwd"
    XW = "xw0 xw1"
    FW = "fw0 fw1"
    QR = " ".join("qr%d" % i for i in range(16))
    dma("s", T.tgs[:], T.tg[:], "", "tgs", 2.7)
    dma("d", T.xw[:, 0:2048], T.xr[:, 0:2048], "", "xw0", 5.0)
    dma("s", T.cxi[:], T.cx[:], "", "cxi", 5.0)
    dma("s", T.q[:], T.qx[:], "", "q", 5.0)
    dma("d", T.xw[:, 2048:W], T.xr[:, 2048:W], "", "xw1", 7.5)
    dma("s", T.lfi[:], T.lf[:], "", "lfi", 9.0)
    dma("d", T.xlh[:], T.xl[:], "", "xlh", 10.5)
    dma("d", T.fdt[:], T.fd[:], "", "fdt", 16.0)
    fill(C("one"), 1.0, "one")
    gop = lambda f, R, Wt: op("g", [f], R, Wt)
    gop(lambda: g.iota(C("pmi", 0, 1), [[0, 1]], 0, 1), "", "pmi")
    gop(lambda: g.affine_select(C("blf"), C("one", 0, 128), [[-16, 8], [0, 16]], Op.is_ge, 0.0, 0, 1), "one", "blf")
    gop(lambda: g.affine_select(C("blf"), C("blf"), [[16, 8], [0, 16]], Op.is_ge, 0.0, 15, -1), "blf", "blf")
    gop(lambda: g.iota(T.ic[:], [[1, 512]], 0, 0), "", "ic")
    gop(lambda: g.affine_select(C("idf"), C("one", 0, 128), [[-1, 128]], Op.is_equal, 0.0, 0, 1), "one", "idf")
    gop(lambda: g.iota(T.ia[:], [[-1, K]], 0, 1), "", "ia")
    gop(lambda: g.affine_select(C("rpf", p1=32), C("one", p1=32), [[-8, 4], [-1, 8], [0, 16]], Op.is_equal, 0.0, 0, 1), "one", "rpf")
    gop(lambda: g.affine_select(C("btf"), C("blf"), [[1, 128]], Op.is_ge, 0.0, 0, -1), "blf", "btf")
    gop(lambda: g.iota(C("dmi"), [[16, 12]], 0, 0), "", "dmi")

    def gaff(t):
        gop(lambda: g.affine_select(C("af%d" % t), C("one", 0, 128), [[-1, 128]], Op.is_equal, 0.0, -(2 + t), 1), "one", "af%d" % t)
    for t in range(RO):
        gaff(t)
    E = lambda i: C("er", i, i + 1)
    b8 = C("blf", st=16)
    ts(C("pmi", 0, 1), C("pmi", 0, 1), 15, Op.bitwise_and, "pmi", "pmi")
    cp(C("pmf", 0, 1), C("pmi", 0, 1), "pmi", "pmf")
    PM = C("pmf", 0, 1)
    ts(T.ic[:], T.ic[:], 15, Op.bitwise_and, "ic", "ic")
    ts(C("sam", 0, 128), T.ic[:, 0:128], 3.0, Op.is_equal, "ic", "sam0")
    tt(C("sa"), C("blf"), C("sam", 0, 128), Op.mult, "blf sam0", "sa")
    for j in range(7):
        ts(E(j), PM, float(j), Op.is_equal, "pmf", "er%d" % j)
    ts(E(8), E(0), 32.0, Op.mult, "er0", "er8")
    ts(E(12), E(3), 32768.0, Op.mult, "er3", "er12")
    tt(E(9), E(8), E(1), Op.add, "er8 er1", "er9")
    ts(E(7), E(3), 65536.0, Op.mult, "er3", "er7")
    ts(E(10), E(9), 2.0, Op.mult, "er9", "er10")
    ts(E(18), E(3), -1.0, Op.mult, "er3", "er18")
    tt(E(11), E(10), E(2), Op.add, "er10 er2", "er11")
    ts(C("lt"), T.ic[:, 0:16], PM, Op.is_gt, "ic pmf", "lt")
    tt(E(13), E(12), E(11), Op.add, "er12 er11", "er13")
    act(C("wm", 0, 8), b8, "blf", "wm", scale=-65536.0)
    act(C("wm", 8, 16), b8, "blf", "wm", scale=-131072.0)
    act(C("wm", 16, 24), b8, "blf", "wm", scale=0.0)
    act(C("wp", 0, 8), b8, "blf er13", "wp", scale=E(13))
    act(C("wp", 8, 16), b8, "blf er7", "wp", scale=E(7))
    act(C("wp", 16, 24), b8, "blf er9", "wp", scale=E(9))
    ts(T.pci[:, 0:256], T.tgs[:], 6, Op.logical_shift_right, "tgs", "pci0")
    ts(T.pci[:, 256:512], T.tgs[:], 1, Op.logical_shift_right, "tgs", "pci1", 31, Op.bitwise_and)
    ts(T.pci[:, 512:768], T.tgs[:], 1, Op.bitwise_and, "tgs", "pci2")
    cp(T.pcs[:], T.pci[:], "pci0 pci1 pci2", "pcs")
    fill(T.pw[:, W:W + K], 0.0, "pwd")
    cp(T.lc[:], T.cxi[:], "cxi", "lc")
    cp(T.cf[:], T.cxi[:], "cxi", "cf")
    ts(T.c16[:], T.cxi[:], -2048.0, Op.add, "cxi", "c16")
    for i in range(16):
        if i % 2:
            act(T.qrep[:, i:16 * K:16], T.q[:], "q", "qr%d" % i)
        else:
            cp(T.qrep[:, i:16 * K:16], T.q[:], "q", "qr%d" % i)
    banks = (("psk0", T.psk[:, 0, :]), ("psk1", T.psk[:, 1, :]), ("psv0", T.psv[:, 0, :]), ("psv1", T.psv[:, 1, :]), ("psm", T.psm[:]), ("psu", T.psu[:]), ("psd", T.psd[:]), ("psg", T.psg[:]))
    for c in range(8):
        bk, ap = banks[c]
        op("p", [mm(ap, C("sa"), T.xw[:, 512 * c:512 * c + 512], True, True)], "sa xw%d" % (c // 4), bk)
        if c % 2:
            cp(T.pw[:, 512 * c:512 * c + 512], ap, bk, "pw%d" % c)
        else:
            act(T.pw[:, 512 * c:512 * c + 512], ap, bk, "pw%d" % c)
    for j in range(3):
        dma("d", T.pw[j:128:16, 0:W], T.pcs[:, 256 * j:256 * j + 256], "pcs " + PWI, "pwr%d" % j, 3.5)

    def weights():
        fill(T.row[:], 0.0, "row")
        ts(T.row[0:1, 0:128], T.ic[0:1, 0:128], 2048.0, Op.mult, "ic", "row")
        ts(T.row[0:1, 128:256], T.ic[0:1, 0:128], 4096.0, Op.mult, "ic", "row", 2048.0, Op.add)
        fill(T.ro2[:], 1.0, "ro2")
        cp(C("idh"), C("idf"), "idf", "idh")

    def scalar_later():
        act(C("idb"), C("idf"), "idf", "idb")
        for nm, cols in (("wm1", (2.0, 0.0, 0.0)), ("wm2", (-2.0, 0.0, 0.0)), ("wp1", (18, 9, 0.0)), ("wp2", (3, 0.0, 9))):
            for j, w in enumerate(cols):
                if w in (18, 9, 3):
                    act(C(nm, 8 * j, 8 * j + 8), b8, "blf er%d" % w, nm, scale=E(w))
                else:
                    act(C(nm, 8 * j, 8 * j + 8), b8, "blf", nm, scale=w)
        act(C("blb"), C("blf"), "blf", "blb")
        act(C("bt"), C("btf"), "btf", "bt")
        for k in range(16):
            act(C("ltk", 128 * k, 128 * k + 128), C("blf"), "blf lt", "ltk", scale=C("lt", k, k + 1))

    def later():
        cp(C("rp", p1=32), C("rpf", p1=32), "rpf", "rp")
        ts(T.ia[:], T.ia[:], 15, Op.bitwise_and, "ia", "ia")
        ts(C("bm"), T.ia[:], 0.0, Op.not_equal, "ia", "bm", BIG, Op.mult)
        ts(T.s0[:], T.ic[:, 0:K], 0.0, Op.is_equal, "ic", "s0", RES, Op.mult)
        for j, w in enumerate((-1.0, -1.0, 2.0)):
            ts(C("bi", 128 * j, 128 * j + 128), C("idf"), w, Op.mult, "idf", "bi")
        ts(T.row[32:33, 384:512], T.ic[32:33, 0:128], 2048.0, Op.mult, "ic row", "row1")

    def latest():
        ts(C("dm4"), C("dmi"), PM, Op.add, "dmi pmf", "dm4", float(W), Op.add)
        ts(C("dm1"), C("dmi"), PM, Op.add, "dmi pmf", "dm1", float(M), Op.add)
        fill(C("exb"), 0.0, "exb")

    def claim_weights():
        ts(T.row[0:1, 384:512], T.ic[0:1, 0:128], 2.0, Op.is_equal, "ic row", "row2")
        for t in range(RO):
            ts(T.row[96:97, 128 * t:128 * t + 128], T.ic[96:97, 0:128], 4.0 + t, Op.is_equal, "ic row", "row3")
        ts(E(14), PM, 4.0, Op.is_ge, "pmf", "er14")
        tt(E(15), E(0), E(1), Op.add, "er0 er1", "er15")
        tt(E(16), E(15), E(14), Op.add, "er15 er14", "er16")
        ts(C("dg1"), C("idf"), E(16), Op.mult, "idf er16", "dg1")
        tt(E(17), E(14), E(3), Op.add, "er14 er3", "er17")
        ts(C("sam", 0, 128), C("idf"), E(17), Op.mult, "idf er17", "sam0")
        for t in range(RO):
            ts(C("af%d" % t), C("af%d" % t), E(4 + t), Op.mult, "af%d er%d" % (t, 4 + t), "af%d" % t)
            tt(C("dgc%d" % t), C("sam", 0, 128), C("af%d" % t), Op.subtract, "sam0 af%d" % t, "dgc%d" % t)
        ts(C("sam", 128, 256), T.ic[:, 0:128], 1.0, Op.is_equal, "ic", "sam1")
        ts(C("vrf", 0, 128), T.ic[:, 0:128], 1.0, Op.is_equal, "ic", "vrf", -32.0, Op.mult)
        ts(C("vrf", 128, 256), T.ic[:, 0:128], 0.0, Op.is_equal, "ic", "vrf1")
        tt(C("sam", 256, 384), C("vrf", 0, 128), C("vrf", 128, 256), Op.add, "vrf vrf1", "sam2")
        tt(C("vrf", 0, 256, p1=32), C("rpf", 256, 512, p1=32), C("sam", 128, 384, p1=32), Op.mult, "rpf sam1 sam2", "vrf vrf1")
        tt(C("vr", p1=32), C("vrf", 0, 128, p1=32), C("vrf", 128, 256, p1=32), Op.add, "vrf", "vr")
        ts(C("vrf", 256, 384, p1=32), C("rpf", 128, 256, p1=32), float(W), Op.mult, "rpf", "vrf2")
        tt(C("rpc", p1=32), C("vrf", 256, 384, p1=32), C("rpf", 0, 128, p1=32), Op.add, "vrf2 rpf", "rpc")

    def yt_weights():
        fill(T.wt[:], 0.0, "wt")
        for c in range(8):
            act(T.wt[:, 64 * c + c:64 * c + 64:8], b8, "blf er11 wt", "wt%d" % c, scale=E(11))

    def disks_out():
        cp(T.lfu[:], T.lfi[:], "lfi", "lfu")
        chip = lambda x: topo.chip(T.cores[x % N])

        def handed(src, j):
            return j > 1 and chip(src - j) == chip(src - j + 1) != chip(src)
        act(C("pb16"), C("idf"), "idf", "pb16", scale=16.0)
        act(C("nb16"), C("idf"), "idf", "nb16", scale=-16.0)
        op("p", [mm(T.psg[:], C("idb"), T.xlh[:, 0:512], True, False), mm(T.psg[:], C("pb16"), T.xlh[:, 512:M], False, True)], "idb pb16 xlh", "psg")
        act(T.xlp[:], T.psg[:], "psg", "xlp")
        for j in (1, 2, 3):
            if not handed(r, j):
                send(T.lfu[:], "lfu", r - j, T["lu%d" % j][:], "rl%d" % j, "ls%d" % (2 * j - 2), True)
            arrives("rl%d" % j, NE, "lu%d" % j, (9.0, 30.0, 40.0)[j - 1])
            if not handed(r, j):
                send(T.xlp[:], "xlp", r - j, T["xp%d" % j][:], "rx%d" % j, "ls%d" % (2 * j - 1), True)
            arrives("rx%d" % j, NE, "xp%d" % j, (13.0, 35.0, 45.0)[j - 1])
        for i in (1, 2):
            if handed(r + i, i + 1):
                send(T["lu%d" % i][:], "lu%d" % i, r - 1, T["lu%d" % (i + 1)][:], "rl%d" % (i + 1), "ls%d" % (10 + 2 * i), True)
                send(T["xp%d" % i][:], "xp%d" % i, r - 1, T["xp%d" % (i + 1)][:], "rx%d" % (i + 1), "ls%d" % (11 + 2 * i), True)

    def features(j):
        x, xl = T["xp%d" % j], T["xl%d" % j]
        act(T.xt[:], x[:], "xp%d" % j, "xt", AF.Copy, scale=0.0625, bias=144.0 - 0.46875)
        act(xl[:, 512:M], T.xt[:], "xt", "xh%d" % j, AF.Copy, bias=-144.0)
        op("p", [mm(T.psg[:], C("idb"), x[:], True, False), mm(T.psg[:], C("nb16"), xl[:, 512:M], False, True)], "idb nb16 xp%d xh%d" % (j, j), "psg")
        act(xl[:, 0:512], T.psg[:], "psg", "xl%d" % j)

    def disk_window(j):
        cp(T["lw%d" % j][:, 0:M], T["lu%d" % j][:], "lu%d" % j, "lw%d" % j)

    def unpack(j):
        if j == 0:
            ts(T.fw[:, 0:2048], T.fdt[:], W - 1, Op.bitwise_and, "fdt", "fw0")
        else:
            ts(T.fw[:, 2048:W], T.fdt[:], 12, Op.logical_shift_right, "fdt", "fw1")

    def apply(buf, win):
        cp(C("lm"), T[buf][:, K:K + 12], buf, "lm")
        cp(T[win][:].indirect(C("lm")), T[buf][:, 0:K], buf + " lm", win)

    EQ = lambda eq: " ".join("%s%d" % (eq, kb) for kb in range(12))

    def same(eq, src, sk, lst, lk):
        for kb in range(11, -1, -1):
            ts(T[eq][:, kb, 0:K - 16 * kb], src[:, 16 * kb:K], C(lst[0], lst[1] + kb, lst[1] + kb + 1), Op.is_equal, sk + " " + lk, eq + str(kb))

    def lower(eq, ps, pk):
        fs = [mm(ps[:, 0:K], C("idb"), C("bm"), True, False)]
        fs += [mm(ps[:, 16 * kb + 16:K], C("blb"), T[eq][:, kb, 16:K - 16 * kb], False, False) for kb in range(10, -1, -1)]
        fs += [mm(ps[:, k:K:16], C("ltk", 128 * k, 128 * k + 128), T[eq][:, :, k], False, k == 15) for k in range(1, 16)]
        op("p", fs, "idb bm blb ltk " + EQ(eq), pk)

    def xgather(dst, lst, lk, h):
        a, b = H * h, H * h + H
        tt(T[dst][:, 16 * a:16 * b], T.xw[:, 0:W].indirect(T[lst][:, a:b]), T.qrep[:, 16 * a:16 * b], Op.min, " ".join((XW, lk, QR)), dst + str(h))

    def pgather(dst, lst, lk, h):
        act(T[dst][:, 16 * H * h:16 * H * (h + 1)], T.pw[:].indirect(T[lst][:, H * h:H * h + H]), PW + " " + lk, dst + str(h))

    def sums(ps, src, w, h, last=False):
        op("p", [mm(T[ps][0:H, h, i:384:16], T[src][:, 16 * H * h + i:16 * H * (h + 1):16], C(w), False, last and i == 15) for i in range(16)],
           "%s%d %s" % (src, h, w), "%s%d" % (ps, h))

    def halves(o, l, R, Wt, n, ident):
        op("p", [mm(o[0:n, H * h:H * h + H], l[0:H, h, 0:n], C(ident, 0, H, p1=H), True, True) for h in (0, 1)], R + " " + ident, Wt)

    def message(t, part):
        msg = "msg%d" % (t + 1)
        if part == 0:
            same("eqt", T.ru[:, 0:K], "rut0 rut1", ("lis", 0), "lisa0 lisa1")
            ts(C("pari"), C("ni"), 1, Op.bitwise_and, "ni0 ni1", "pari")
            ts(C("w5"), C("pari"), -2.0, Op.mult, "pari", "w5", 1.0, Op.add)
            tt(C("w6"), C("w5"), C("ni"), Op.add, "w5 ni0 ni1", "w6")
            tt(C("w5"), C("w6"), C("dm1"), Op.subtract, "w6 dm1", "w5")
            return
        lower("eqt", T.psd, "psd")
        scan(T.sct2[:], T.psd[:, 0:K], "psd", "sct2")
        ts(C("z", 12, 24), T.sct2[:, 15:K:16], 0.0, Op.is_equal, "sct2", "z1")
        tt(C("dwin"), C("req"), C("z", 12, 24), Op.mult, "req z1", "dwin")
        tt(C("w6"), C("w5"), C("dwin"), Op.mult, "w5 dwin", "w6")
        tt(T[msg][:, K:K + 12], C("w6"), C("dm1"), Op.add, "w6 dm1", msg + "l")
        mk = msg + " " + msg + "l"
        if t == 0:
            send(T[msg][:], mk, r - 1, T.up1[:], "ru1", "ls6")
            arrives("ru1", NE, "up1", 7.0)
            send(T[msg][:], mk, r - 2, T.up2[:], "ru2", "ls7")
            arrives("ru2", NE, "up2", 20.0)
        elif t == 1:
            send(T[msg][:], mk, r - 1, T.up3[:], "ru3", "ls8")
            arrives("ru3", NE, "up3", 7.0)
        send(T[msg][:], mk, r + 1 + t, T["hm%d" % (t + 1)][:], "rh%d" % (t + 1), "ls%d" % (9 + t))
        arrives("rh%d" % (t + 1), NE, "hm%d" % (t + 1), (50.0, 20.0, 8.0)[t])

    L = lambda n: T[n][0:H, :, :]
    X = lambda n, i: T[n][0:H, :, 8 * i:8 * i + 8]
    for t in range(RO):
        j = t + 1
        lw, xl, msg = "lw%d" % j, "xl%d" % j, "msg%d" % j
        if t == 0:
            scalar_later()
        if t == 0:
            disks_out()
            weights()
            later()
            latest()
            claim_weights()
            unpack(0)
            unpack(1)
            disk_window(1)
        elif t == 1:
            disk_window(2)
            disk_window(3)
            apply("up1", "lw2")
            apply("up2", "lw3")
        else:
            apply("up3", "lw3")
            cp(T.lh[:, 0:M], T.lfi[:], "lfi", "lh")
        if t:
            ts(T.c16[:], T.cf[:], -2048.0, Op.add, "cf", "c16")
        R16 = lambda f: C("rp", 128 * f, 128 * f + 128, p1=16)
        lnw = T[lw][:, 0:M]
        for h in (0, 1):
            a, b, x, y = H * h, H * h + H, 6 * h, 6 * h + 6
            k = lambda names: " ".join("%s%d" % (n, h) for n in names.split())
            pgather("pa", "lc", "lc", h)
            xgather("ma", "lc", "lc", h)
            op("p", [mm(T.psk[0:H, h, 0:384], T.ro2[0:1, 0:H], T.row[0:1, 0:384], True, False)], "ro2 row", k("psk"))
            sums("psk", *(("pa", "wp") if t else ("ma", "wm")), h)
            sums("psk", *(("ma", "wm") if t else ("pa", "wp")), h)
            op("p", [mm(T.psk[0:H, h, 128:256], T.c16[:, a:b], C("idh"), False, True)], "c16 idh", k("psk"))
            act(T.co[0:H, h, :], T.psk[0:H, h, 1:256:2], k("psk"), k("co"))
            tt(T.t1[0:H, h, :], T.psk[0:H, h, 0:256:2], T.co[0:H, h, :], Op.min, k("psk co"), k("t1_"))
            act(T.sl[0:H, h, :], T.psk[0:H, h, 256:384], k("psk"), k("sl"))
            tt(T.t2[0:H, h, :], T.t1[0:H, h, 0:128:2], T.t1[0:H, h, 1:128:2], Op.min, k("t1_"), k("t2_"))
            tt(T.t3[0:H, h, :], T.t2[0:H, h, 0:64:2], T.t2[0:H, h, 1:64:2], Op.min, k("t2_"), k("t3_"))
            tt(T.t4[0:H, h, :], T.t3[0:H, h, 0:32:2], T.t3[0:H, h, 1:32:2], Op.min, k("t3_"), k("t4_"))
            ts(T.fi[0:H, h, 8:16], T.t4[0:H, h, 8:16], W - 1, Op.bitwise_and, k("t4_"), k("fio"))
            ts(T.fi[0:H, h, 0:8], T.t4[0:H, h, 0:8], 2047, Op.bitwise_and, k("t4_"), k("fit"))
            ts(T.fl[0:H, h, 8:16], T.fi[0:H, h, 8:16], -2048.0, Op.add, k("fio"), k("flo"))
            cp(T.fl[0:H, h, 0:8], T.fi[0:H, h, 0:8], k("fit"), k("flt"))
            op("p", [mm(T.psk[0:16, h, 384:480], T.fl[0:H, h, :], C("idh", 0, H, p1=H), True, True)], k("flo flt") + " idh", k("psk"))
            cp(T.gt[0:16, a:b], T.psk[0:16, h, 384:480], k("psk"), k("gt"))
            pb, pk = ((T.psm, "psm"), (T.psu, "psu"))[h]
            fs = []
            for f in (0, 1):
                fs += [mm(pb[:, H * f:H * f + H], R16(f), T.gt[0:16, a:b], True, False), mm(pb[:, H * f:H * f + H], C("idb"), C("bm", 0, H), False, True),
                       mm(pb[:, H * f + K:H * f + K + H], R16(f), T.gt[0:16, a:b], True, True)]
            op("p", fs, "rp idb bm " + k("gt"), pk)
            scan(T.sct[:, a:b], pb[:, 0:H], pk, k("sct"), H)
            ts(C("ni", x, y), T.sct[:, a + 15:b:16], 1, Op.logical_shift_right, k("sct"), k("ni"))
            cp(C("ln", x, y), C("ni", x, y), k("ni"), k("ln"))
            LN = C("ln", x, y)
            act(T.sq[:, a:b], lnw.indirect(LN), lw + " " + k("ln"), k("sqa"), AF.Square, bias=4.0)
            act(T.sq[:, K + a:K + b], lnw.indirect(LN), lw + " " + k("ln"), k("sqb"), AF.Square, bias=592.0)
            cp(T.b16[:, a:b], lnw.indirect(LN), lw + " " + k("ln"), k("b16_"))
            if h == 0:
                features(j)
            act(T.at[:, a:b], T[xl][:].indirect(LN), xl + " xh%d " % j + k("ln"), k("at"))
            for c, (sc, of) in enumerate(((0.125, -2.4375), (0.03125, -10951.484375))):
                u, w, n = K * c + a, K * c + b, "ab"[c]
                ts(T.tt[:, u:w], T.sq[:, u:w], sc, Op.mult, k("sq" + n), k("tt" + n), of, Op.add)
                ts(T.cc[:, u:w], T.tt[:, u:w], W - 1, Op.bitwise_and, k("tt" + n), k("cc" + n))
                cp(T["l%d" % (c + 1)][:, a:b], T.cc[:, u:w], k("cc" + n), k("li" + n))
            scan(T.sco[:, a:b], pb[:, H:K], pk, k("sco"), H)
            ts(T.ru[:, a:b], pb[:, K:K + H], 2048.0, Op.add, pk, k("rut"))
            ts(T.ru[:, K + a:K + b], pb[:, K + H:2 * K], 2048.0, Op.add, pk, k("ruo"))
            ts(C("lis", 12 + x, 12 + y), T.sco[:, a + 15:b:16], 2048.0, Op.add, k("sco"), k("lisb"))
            ts(C("lis", x, y), T.sct[:, a + 15:b:16], 2048.0, Op.add, k("sct"), k("lisa"))
            op("p", [mm(T.psv[0:H, h, :], T.ro2[32:33, 0:H], T.row[32:33, :], True, False),
                     mm(T.psv[0:H, h, 128:512], T.b16[:, a:b], C("bi"), False, False)], "ro2 row1 bi " + k("b16_"), k("psv"))
        for h in (0, 1):
            for c in "ab":
                pgather("p" + c, "l%d" % ("ab".index(c) + 1), "li%s%d" % (c, h), h)
                xgather("m" + c, "l%d" % ("ab".index(c) + 1), "li%s%d" % (c, h), h)
                sums("psv", "m" + c, "wm%d" % ("ab".index(c) + 1), h)
                sums("psv", "p" + c, "wp%d" % ("ab".index(c) + 1), h, c == "b")
        cp(C("lo"), C("lis", 12, 24), "lisb0 lisb1", "lo")
        same("eqo", T.ru[:, K:2 * K], "ruo0 ruo1", ("lis", 12), "lisb0 lisb1")
        lower("eqo", T.psd, "psd")
        message(t, 0)
        scan(T.scd[:], T.psd[:, 0:K], "psd", "scd")
        ts(C("ei"), T.sct[:, 15:K:16], 1, Op.bitwise_and, "sct0 sct1", "ei")
        ts(C("z", 0, 12), T.scd[:, 15:K:16], 0.0, Op.is_equal, "scd", "z0")
        tt(C("w1"), C("lis", 12, 24), C("dm4"), Op.subtract, "lisb0 lisb1 dm4", "w1")
        tt(C("cand"), C("z", 0, 12), C("ei"), Op.mult, "z0 ei", "cand")
        op("v", [lambda: v.tensor_tensor_scan(C("exb", 1, 13), C("one", 0, 12), C("cand"), 0.0, Op.mult, Op.add)], "one cand", "exb")
        op("p", [mm(T.psg[:, 400:412], C("bt"), C("cand"), True, False), mm(T.psg[:, 400:412], C("blb"), C("exb", 0, 12), False, True)], "bt cand blb exb", "psg")
        ts(C("rk"), T.psg[:, 400:412], float(CAP), Op.is_le, "psg", "rk")
        halves(T.psk[:, 1, :], T.sl, "sl0 sl1", "psk1", 128, "idf")
        tt(T.dc[:], T.cc[:, K:2 * K], T.cc[:, 0:K], Op.subtract, "cca0 cca1 ccb0 ccb1", "dc")
        tt(C("req"), C("rk"), C("cand"), Op.mult, "rk cand", "req")
        tt(C("w2"), C("w1"), C("req"), Op.mult, "w1 req", "w2")
        ts(C("nrq"), C("req"), -8192.0, Op.mult, "req", "nrq", 8192.0 + 2048.0, Op.add)
        tt(C("ld"), C("w2"), C("dm4"), Op.add, "w2 dm4", "ld")
        act(T[msg][:, 0:K], T.psk[:, 1, 0:K], "psk1", msg)
        message(t, 1)
        act(T.g2[:], T.pw[:].indirect(C("ld")), PW + " ld", "g2")
        op("p", [mm(T.psk[:, 0, 0:K], C("sa"), T.at[:], True, False), mm(T.psk[:, 0, 0:K], C("dg1"), T.g2[:], False, False),
                 mm(T.psk[:, 0, 0:K], T.row[96:97, 128 * t:128 * t + 128], T.ro2[96:97, 0:K], False, True)], "sa at0 at1 dg1 g2 row3 ro2", "psk0")
        act(T.v2[:], T.psk[:, 0, 0:K], "psk0", "v2")
        cp(T.xw[:].indirect(C("ld")), T.at[:], "ld at0 at1", XW)
        for h in (0, 1):
            k = lambda names: " ".join("%s%d" % (n, h) for n in names.split())
            U = lambda n: T[n][0:H, h, :]
            ts(U("r1"), T.psv[0:H, h, 128:256], 0.0, Op.is_equal, k("psv"), k("ra"), -4096.0, Op.mult)
            ts(T.psv[0:H, h, 256:384], T.psv[0:H, h, 256:384], 0.0, Op.is_equal, k("psv"), k("rb psv"), 1024.0, Op.mult)
            tt(U("u1"), T.psv[0:H, h, 0:128], U("r1"), Op.add, k("psv ra"), k("ua"))
            tt(U("u2"), T.psv[0:H, h, 256:384], U("u1"), Op.add, k("psv ua rb"), k("uc"))
            act(U("ub"), U("u2"), k("uc"), k("ub"), AF.Abs)
            ts(U("pk"), U("u2"), 0.0, Op.is_gt, k("uc"), k("pk"))
            tt(U("kk"), T.psv[0:H, h, 384:512], U("pk"), Op.add, k("psv pk"), k("kk"))
            ts(T.psv[0:H, h, 128:256], U("ub"), 512.0, Op.is_gt, k("ub ra"), k("rc psv"), RES, Op.mult)
            tt(U("k2"), T.psv[0:H, h, 128:256], U("kk"), Op.add, k("psv kk rc"), k("kz"))
            tt(U("ka"), T.k2[0:H, h, 0:128:2], T.k2[0:H, h, 1:128:2], Op.min, k("kz"), k("ka"))
            tt(U("kb"), T.ka[0:H, h, 0:64:2], T.ka[0:H, h, 1:64:2], Op.min, k("ka"), k("kb"))
            tt(U("kc"), T.kb[0:H, h, 0:32:2], T.kb[0:H, h, 1:32:2], Op.min, k("kb"), k("kc"))
            tt(U("kd"), T.kc[0:H, h, 0:16:2], T.kc[0:H, h, 1:16:2], Op.min, k("kc"), k("kd"))
        halves(T.psg, T.pk, "pk0 pk1", "psg", 128, "idb")
        KD = "kd0 kd1"
        ts(X("t7", 0), L("kd"), 1, Op.logical_shift_right, KD, "t7", 1023, Op.bitwise_and)
        ts(X("t7", 1), L("kd"), 6, Op.logical_shift_right, KD, "t7p", 31, Op.bitwise_and)
        ts(X("fg", 0), X("t7", 0), 4.0, Op.add, "t7", "fga")
        ts(X("fg", 1), X("t7", 0), 592.0, Op.add, "t7", "fgb")
        ts(X("fh", 0), L("kd"), 1, Op.bitwise_and, KD, "fh")
        tt(L("t5"), L("fg"), L("fg"), Op.mult, "fga fgb", "t5")
        cp(T.fm[0:H, :, 16:32], L("t7"), "t7 t7p", "fm1")
        ts(X("fj", 0), X("t5", 0), 0.125, Op.mult, "t5", "fja", -2.4375, Op.add)
        ts(X("fj", 1), X("t5", 1), 0.03125, Op.mult, "t5", "fjb", -10951.484375, Op.add)
        ts(X("fm", 1), L("kd"), RES, Op.is_ge, KD, "fm2")
        ts(L("fe"), L("fj"), W - 1, Op.bitwise_and, "fja fjb", "fe")
        tt(X("t6", 1), X("fe", 1), X("fe", 0), Op.subtract, "fe", "t6")
        ts(X("t6", 0), X("fe", 0), -2048.0, Op.add, "fe", "t6b")
        tt(X("t6", 2), X("t6", 1), X("fh", 0), Op.mult, "t6 fh", "t6c")
        tt(X("fm", 0), X("t6", 2), X("t6", 0), Op.add, "t6c t6b", "fm0")
        halves(T.psm, T.fm, "fm0 fm1 fm2", "psm", 32, "idh")
        tt(T.sp[:], T.psg[:, 0:K], T.dc[:], Op.mult, "psg dc", "sp")
        cp(T.gu[0:32, :], T.psm[0:32, 0:K], "psm", "gu")
        op("p", [mm(T.psu[:, 0:K], C("rpc", p1=32), T.gu[0:32, :], True, True)], "rpc gu", "psu")
        op("p", [mm(T.psg[:, 0:K], C("rpc", p1=32), T.gu[0:32, :], True, False), mm(T.psg[:, 0:K], C("idb"), C("bm"), False, True)], "rpc gu idb bm", "psg")
        tt(T.sg[:], T.sp[:], T.cc[:, 0:K], Op.add, "sp cca0 cca1", "sg")
        cp(T.pw[:].indirect(C("ld")), T.v2[:], "ld v2", PW)
        ts(T.ru2[:], T.psu[:, 0:K], 2048.0, Op.add, "psu", "ru2_")
        scan(T.scl[:], T.psg[:, 0:K], "psg", "scl")
        tt(C("pls"), C("nrq"), T.scl[:, 15:K:16], Op.add, "nrq scl", "pls")
        same("eqo", T.ru2, "ru2_", ("pls", 0), "pls")
        lower("eqo", T.psd, "psd")
        ts(C("w3"), C("pls"), float(W), Op.is_lt, "pls", "w3")
        tt(C("w4"), C("pls"), C("dm4"), Op.subtract, "pls dm4", "w4")
        cp(T.fw[:].indirect(C("ld")), T.sg[:], "ld sg", FW)
        tt(C("w2"), C("w3"), C("w4"), Op.mult, "w3 w4", "w2")
        tt(T.qs[:], T.xw[:, 0:W].indirect(C("lo")), T.q[:], Op.add, XW + " lo q", "qs")
        cp(T.cf[:], T.fw[:, 0:W].indirect(C("lo")), FW + " lo", "cf")
        ts(T.qb[:], T.qs[:], 0.5, Op.mult, "qs", "qb", 127.8125, Op.add)
        if t < RO - 1:
            cp(T.lc[:], T.cf[:], "cf", "lc")
            for i in range(16):
                ts(T.qrep[:, i:16 * K:16], T.qb[:], -128.0, Op.add, "qb", "qr%d" % i)
        ts(T.q[:], T.qb[:], -128.0, Op.add, "qb", "q")
        scan(T.scd[:], T.psd[:, 0:K], "psd", "scd")
        ts(C("z", 0, 12), T.scd[:, 15:K:16], 0.0, Op.is_equal, "scd", "z0")
        tt(C("w1"), C("w2"), C("z", 0, 12), Op.mult, "w2 z0", "w1")
        tt(C("lcl"), C("w1"), C("dm4"), Op.add, "w1 dm4", "lcl")
        act(T.g1[:], T.pw[:].indirect(C("lcl")), PW + " lcl", "g1")
        op("p", [mm(T.psm[:, 0:K], C("vr", p1=32), T.gu[0:32, :], True, False),
                 mm(T.psm[:, 0:K], T.row[0:1, 384:512], T.ro2[0:1, 0:K], False, False),
                 mm(T.psm[:, 0:K], C("dgc%d" % t), T.g1[:], False, True)], "vr gu row2 ro2 dgc%d g1" % t, "psm")
        act(T.v1[:], T.psm[:, 0:K], "psm", "v1")
        cp(T.pw[:].indirect(C("lcl")), T.v1[:], "lcl v1", PW)
        if t == 1:
            yt_weights()
    dma("d", T.yc[:], T.cf[:], "cf", "yc")
    dma("d", T.yq[:], T.q[:], "q", "yq")
    op("p", [mm(T.psv[0:64, 0, :], T.wt[:, 64 * c:64 * c + 64], T.pw[:, 512 * c:512 * c + 512], c == 0, c == 7) for c in range(8)], " ".join("wt%d" % c for c in range(8)) + " " + PW, "psv0")
    for j in (1, 2, 3):
        apply("hm%d" % j, "lh")
    act(T.yts[0:64, :], T.psv[0:64, 0, :], "psv0", "yts")
    dma("d", T.yt[:], T.yts[0:64, :], "yts", "yt")
    dma("d", T.yl[:], T.lh[:, 0:M], "lh", "yl")
    finish()
